import numpy as np
import ml_dtypes


def mxq(x, axis, fmt="e4m3"):
    dtype, down = {"e4m3": (ml_dtypes.float8_e4m3fn, 7), "e5m2": (ml_dtypes.float8_e5m2, 14)}[fmt]
    v = np.moveaxis(np.asarray(x, np.float32).astype(ml_dtypes.bfloat16).astype(np.float64), axis, -1)
    blocks = v.reshape(v.shape[:-1] + (-1, 32))
    amax = np.abs(blocks).max(-1, keepdims=True)
    byte = np.maximum(np.where(amax > 0, np.frexp(amax)[1] - 1 + 127, 0) - down, 1)
    scale = np.exp2(byte - 127.0)
    codes = (blocks / scale).astype(np.float32).astype(dtype).astype(np.float64)
    return np.moveaxis((codes * scale).reshape(v.shape), -1, axis)


WIDE = False


def mx_kscale(k):
    if not WIDE:
        return np.ones(k)
    levels = np.array([10, -10, 5, -5, 0])
    if k % 512:
        return np.exp2(np.random.permutation(np.resize(levels, k // 32))).repeat(32)
    a = np.empty((k // 512, 16))
    for p in range(k // 512):
        a[p, :8] = np.random.permutation(np.resize(levels, 8))
        for g in range(8):
            far = levels[np.abs(levels - a[p, g]) >= 10]
            a[p, g + 8] = far[np.random.randint(len(far))]
    return np.exp2(a.ravel()).repeat(32)


def f64(x):
    return np.asarray(x).astype(np.float64)


def striped(idx):
    return np.tile(np.asarray(idx).reshape(-1, 16).T, (8, 1)).astype(np.uint16)


def unstriped(offs):
    return offs[:16].T.reshape(-1).astype(np.int64)


G, K, T, D, M = 128, 4, 1024, 512, 256


def setup_inputs():
    n = np.random.standard_normal
    s = mx_kscale(D)[:, None]
    x = n((D, T)) * s
    idx = np.random.permutation(T)[:G * K].reshape(G, K)
    return {
        "xT": x.astype(np.float32),
        "w": (n((D, M)) / np.sqrt(D) / s).astype(np.float32),
        "bias": (0.3 * n((M, 1))).astype(np.float32),
        "offs": striped(idx.reshape(-1)),
    }


def reference(xT, w, bias, offs):
    x = f64(xT)[:, unstriped(offs)]
    y = (mxq(f64(w), 0, "e4m3").T @ mxq(x, 0, "e4m3")).reshape(M, G, K).max(-1)
    y = y + f64(bias)
    return y

@@ -1,0 +1,138 @@
+import concourse.mybir as mybir
+
+F32 = mybir.dt.float32
+BF16 = mybir.dt.bfloat16
+U32 = mybir.dt.uint32
+U16 = mybir.dt.uint16
+U8 = mybir.dt.uint8
+FP8X4 = mybir.dt.float8_e4m3fn_x4
+COPY = mybir.ActivationFunctionType.Copy
+IDENTITY = mybir.ActivationFunctionType.Identity
+MAX = mybir.AluOpType.max
+AXIS_X = mybir.AxisListType.X
+
+P = 128
+PACK = 4
+G, K, T, D, M = 128, 4, 1024, 512, 256
+N = G * K
+FLOPS = 2 * D * M * N
+
+
+def tile_attend_edge_uniq_bias_kernel(tc, xT, w, bias, offs, out):
+    nc = tc.nc
+    x_rows = xT.rearrange("(p t) c -> p t c", t=PACK)
+    w_rows = w.rearrange("(p t) m -> p t m", t=PACK)
+    out_rows = out.rearrange("(p h) g -> p h g", h=2)
+    half = N // 2
+    half_g = G // 2
+
+    with (
+        tc.tile_pool(name="held", bufs=1) as held,
+        tc.psum_pool(name="psum", bufs=1) as psum,
+    ):
+        offsets = held.tile([P, N // 16], U16, name="offsets")
+        raw_a = held.tile([P, 2, T], F32, name="raw_a", align_bytes=64)
+        raw_b = held.tile([P, 2, T], F32, name="raw_b", align_bytes=64)
+        raw_w = held.tile([P, PACK, M], F32, name="raw_w", align_bytes=64)
+        bias_cols = held.tile([P, 2], F32, name="bias_cols")
+
+        nc.sync.dma_start(raw_a[:, :, 0:768], x_rows[:, 0:2, 0:768])
+        nc.sync.dma_start(raw_a[:, :, 768:1024], x_rows[:, 0:2, 768:1024])
+        nc.sync.dma_start(offsets[:], offs)
+        nc.sync.dma_start(raw_b[:, :, 0:512], x_rows[:, 2:4, 0:512])
+        nc.sync.dma_start(raw_b[:, :, 512:832], x_rows[:, 2:4, 512:832])
+        nc.sync.dma_start(raw_b[:, :, 832:1024], x_rows[:, 2:4, 832:1024])
+        nc.sync.dma_start(raw_w[:], w_rows)
+        nc.sync.dma_start(bias_cols[:], bias.rearrange("(p h) o -> p (h o)", h=2))
+
+        pair_a = held.tile([P, T, 2], BF16, name="pair_a", align_bytes=64)
+        pair_b = held.tile([P, T, 2], BF16, name="pair_b", align_bytes=64)
+        w_grouped = held.tile([P, 2, P, PACK], BF16, name="w_grouped", align_bytes=64)
+        x_grouped = held.tile([P, N, PACK], BF16, name="x_grouped", align_bytes=64)
+        x_codes = held.tile([P, N], U32, name="x_codes", align_bytes=64)
+        x_scales = held.tile([P, N], U8, name="x_scales", align_bytes=64)
+        w_codes = held.tile([P, M], U32, name="w_codes", align_bytes=64)
+        w_scales = held.tile([P, M], U8, name="w_scales", align_bytes=64)
+
+        def pair_view(raw, lo, hi):
+            return raw[:, :, lo:hi].rearrange("p t c -> p c t")
+
+        a_words = pair_a[:].rearrange("p c t -> p (c t)").bitcast(U32)
+        b_words = pair_b[:].rearrange("p c t -> p (c t)").bitcast(U32)
+        x_words = x_grouped[:].rearrange("p c t -> p (c t)").bitcast(U32).rearrange("p (c u) -> p c u", u=2)
+        x_flat = x_grouped[:].rearrange("p c t -> p (c t)")
+
+        def cast_v(pair, raw, lo, hi):
+            nc.vector.tensor_copy(pair[:, lo:hi, :], pair_view(raw, lo, hi))
+
+        def cast_s(pair, raw, lo, hi):
+            nc.scalar.activation(pair[:, lo:hi, :], pair_view(raw, lo, hi), COPY)
+
+        cast_v(pair_a, raw_a, 0, 512)
+        cast_s(pair_a, raw_a, 512, 768)
+        cast_v(pair_a, raw_a, 768, 936)
+        cast_s(pair_a, raw_a, 936, 1024)
+        nc.vector.tensor_copy(x_words[:, :, 0], a_words.indirect(offsets[:]))
+        cast_s(pair_b, raw_b, 0, 512)
+        cast_v(pair_b, raw_b, 512, 832)
+        cast_v(pair_b, raw_b, 832, 944)
+        cast_s(pair_b, raw_b, 944, 1024)
+        for h in range(2):
+            nc.scalar.activation(w_grouped[:, h, :, :], raw_w[:].rearrange("p t (m h) -> p h m t", h=2)[:, h, :, :], COPY)
+        for i in range(2):
+            nc.vector.tensor_copy(
+                x_words[:, half * i : half * i + half, 1],
+                b_words.indirect(offsets[:, 16 * i : 16 * i + 16]),
+            )
+        nc.vector.quantize_mx(x_codes[:, 0:half].bitcast(FP8X4), x_scales[:, 0:half], x_flat[:, 0 : 4 * half])
+        for h in range(2):
+            nc.vector.quantize_mx(
+                w_codes[:, P * h : P * h + P].bitcast(FP8X4),
+                w_scales[:, P * h : P * h + P],
+                w_grouped[:, h, :, :].rearrange("p m t -> p (m t)"),
+            )
+        nc.vector.quantize_mx(x_codes[:, half:N].bitcast(FP8X4), x_scales[:, half:N], x_flat[:, 4 * half : 4 * N])
+
+        def multiply(h, lo, hi):
+            acc = psum.tile([P, hi - lo], F32, name=f"acc_{h}_{lo}")
+            nc.tensor.matmul_mx(
+                out=acc[:],
+                lhsT=w_codes[:, P * h : P * h + P].bitcast(FP8X4),
+                lhsT_scale=w_scales[:, P * h : P * h + P],
+                rhs=x_codes[:, lo:hi].bitcast(FP8X4),
+                rhs_scale=x_scales[:, lo:hi],
+                start=True,
+                stop=True,
+            )
+            return acc
+
+        def largest(top, acc):
+            nc.vector.tensor_reduce(top, acc[:].rearrange("p (g j) -> p g j", j=K), AXIS_X, MAX)
+
+        def add_bias(res, top, h):
+            nc.scalar.activation(res, top, IDENTITY, bias=bias_cols[:, h : h + 1])
+
+        acc_00 = multiply(0, 0, 256)
+        acc_10 = multiply(1, 0, 256)
+        acc_01 = multiply(0, 256, 512)
+        acc_11 = multiply(1, 256, 384)
+        acc_12 = multiply(1, 384, 512)
+        tops = []
+        ress = []
+        for i in range(2):
+            top = held.tile([P, 2, half_g], F32, name=f"top_{i}")
+            res = held.tile([P, 2, half_g], F32, name=f"res_{i}")
+            tops.append(top)
+            ress.append(res)
+        largest(tops[0][:, 0, :], acc_00)
+        add_bias(ress[0][:, 0, :], tops[0][:, 0, :], 0)
+        largest(tops[0][:, 1, :], acc_10)
+        add_bias(ress[0][:, 1, :], tops[0][:, 1, :], 1)
+        nc.sync.dma_start(out_rows[:, :, 0:half_g], ress[0][:])
+        largest(tops[1][:, 0, :], acc_01)
+        add_bias(ress[1][:, 0, :], tops[1][:, 0, :], 0)
+        nc.sync.dma_start(out_rows[:, 0, half_g:G], ress[1][:, 0, :])
+        largest(tops[1][:, 1, 0:32], acc_11)
+        largest(tops[1][:, 1, 32:64], acc_12)
+        add_bias(ress[1][:, 1, :], tops[1][:, 1, :], 1)
+        nc.sync.dma_start(out_rows[:, 1, half_g:G], ress[1][:, 1, :])

@@ -16,6 +16,8 @@ PACK = 4
 G, K, T, D, M = 128, 4, 1024, 512, 256
 N = G * K
 FLOPS = 2 * D * M * N
+CAST_SPLIT = 640
+ENTRY_SPLIT = 384
 
 
 def tile_attend_edge_uniq_bias_kernel(tc, xT, w, bias, offs, out):
@@ -31,22 +33,20 @@ def tile_attend_edge_uniq_bias_kernel(tc, xT, w, bias, offs, out):
         tc.psum_pool(name="psum", bufs=1) as psum,
     ):
         offsets = held.tile([P, N // 16], U16, name="offsets")
-        raw_a = held.tile([P, 2, T], F32, name="raw_a", align_bytes=64)
-        raw_b = held.tile([P, 2, T], F32, name="raw_b", align_bytes=64)
+        raw = [held.tile([P, T], F32, name=f"raw_{t}", align_bytes=64) for t in range(PACK)]
         raw_w = held.tile([P, PACK, M], F32, name="raw_w", align_bytes=64)
         bias_cols = held.tile([P, 2], F32, name="bias_cols")
 
-        nc.sync.dma_start(raw_a[:, :, 0:768], x_rows[:, 0:2, 0:768])
-        nc.sync.dma_start(raw_a[:, :, 768:1024], x_rows[:, 0:2, 768:1024])
+        nc.sync.dma_start(raw[2][:], x_rows[:, 2, :])
         nc.sync.dma_start(offsets[:], offs)
-        nc.sync.dma_start(raw_b[:, :, 0:512], x_rows[:, 2:4, 0:512])
-        nc.sync.dma_start(raw_b[:, :, 512:832], x_rows[:, 2:4, 512:832])
-        nc.sync.dma_start(raw_b[:, :, 832:1024], x_rows[:, 2:4, 832:1024])
+        nc.sync.dma_start(raw[0][:], x_rows[:, 0, :])
+        nc.sync.dma_start(raw[3][:], x_rows[:, 3, :])
+        nc.sync.dma_start(raw[1][:], x_rows[:, 1, :])
         nc.sync.dma_start(raw_w[:], w_rows)
         nc.sync.dma_start(bias_cols[:], bias.rearrange("(p h) o -> p (h o)", h=2))
 
-        pair_a = held.tile([P, T, 2], BF16, name="pair_a", align_bytes=64)
-        pair_b = held.tile([P, T, 2], BF16, name="pair_b", align_bytes=64)
+        cast_2 = held.tile([P, T], BF16, name="cast_2", align_bytes=64)
+        cast_3 = held.tile([P, T], BF16, name="cast_3", align_bytes=64)
         w_grouped = held.tile([P, 2, P, PACK], BF16, name="w_grouped", align_bytes=64)
         x_grouped = held.tile([P, N, PACK], BF16, name="x_grouped", align_bytes=64)
         x_codes = held.tile([P, N], U32, name="x_codes", align_bytes=64)
@@ -54,36 +54,27 @@ def tile_attend_edge_uniq_bias_kernel(tc, xT, w, bias, offs, out):
         w_codes = held.tile([P, M], U32, name="w_codes", align_bytes=64)
         w_scales = held.tile([P, M], U8, name="w_scales", align_bytes=64)
 
-        def pair_view(raw, lo, hi):
-            return raw[:, :, lo:hi].rearrange("p t c -> p c t")
-
-        a_words = pair_a[:].rearrange("p c t -> p (c t)").bitcast(U32)
-        b_words = pair_b[:].rearrange("p c t -> p (c t)").bitcast(U32)
-        x_words = x_grouped[:].rearrange("p c t -> p (c t)").bitcast(U32).rearrange("p (c u) -> p c u", u=2)
         x_flat = x_grouped[:].rearrange("p c t -> p (c t)")
 
-        def cast_v(pair, raw, lo, hi):
-            nc.vector.tensor_copy(pair[:, lo:hi, :], pair_view(raw, lo, hi))
+        def gather_v(t, lo, hi):
+            nc.vector.tensor_copy(x_grouped[:, lo:hi, t], raw[t][:].indirect(offsets[:, lo // 16 : hi // 16]))
 
-        def cast_s(pair, raw, lo, hi):
-            nc.scalar.activation(pair[:, lo:hi, :], pair_view(raw, lo, hi), COPY)
+        def gather_s(t, cast, lo, hi):
+            nc.scalar.activation(x_grouped[:, lo:hi, t], cast[:].indirect(offsets[:, lo // 16 : hi // 16]), COPY)
 
-        cast_v(pair_a, raw_a, 0, 512)
-        cast_s(pair_a, raw_a, 512, 768)
-        cast_v(pair_a, raw_a, 768, 936)
-        cast_s(pair_a, raw_a, 936, 1024)
-        nc.vector.tensor_copy(x_words[:, :, 0], a_words.indirect(offsets[:]))
-        cast_s(pair_b, raw_b, 0, 512)
-        cast_v(pair_b, raw_b, 512, 832)
-        cast_v(pair_b, raw_b, 832, 944)
-        cast_s(pair_b, raw_b, 944, 1024)
+        nc.scalar.activation(cast_2[:, 0:256], raw[2][:, 0:256], COPY)
+        nc.vector.tensor_copy(cast_2[:, 256:T], raw[2][:, 256:T])
+        gather_s(2, cast_2, 0, ENTRY_SPLIT)
+        gather_v(2, ENTRY_SPLIT, N)
+        gather_v(0, 0, N)
+        nc.scalar.activation(cast_3[:, 0:CAST_SPLIT], raw[3][:, 0:CAST_SPLIT], COPY)
+        nc.vector.tensor_copy(cast_3[:, CAST_SPLIT:T], raw[3][:, CAST_SPLIT:T])
+        gather_s(3, cast_3, 0, ENTRY_SPLIT)
+        gather_v(3, ENTRY_SPLIT, N)
         for h in range(2):
             nc.scalar.activation(w_grouped[:, h, :, :], raw_w[:].rearrange("p t (m h) -> p h m t", h=2)[:, h, :, :], COPY)
         for i in range(2):
-            nc.vector.tensor_copy(
-                x_words[:, half * i : half * i + half, 1],
-                b_words.indirect(offsets[:, 16 * i : 16 * i + 16]),
-            )
+            gather_v(1, half * i, half * i + half)
         nc.vector.quantize_mx(x_codes[:, 0:half].bitcast(FP8X4), x_scales[:, 0:half], x_flat[:, 0 : 4 * half])
         for h in range(2):
             nc.vector.quantize_mx(

@@ -17,14 +17,14 @@ G, K, T, D, M = 128, 4, 1024, 512, 256
 N = G * K
 FLOPS = 2 * D * M * N
 CAST_SPLIT = 640
-ENTRY_SPLIT = 384
+ENTRY_SPLIT = 352
 
 
 def tile_attend_edge_uniq_bias_kernel(tc, xT, w, bias, offs, out):
     nc = tc.nc
     x_rows = xT.rearrange("(p t) c -> p t c", t=PACK)
     w_rows = w.rearrange("(p t) m -> p t m", t=PACK)
-    out_rows = out.rearrange("(p h) g -> p h g", h=2)
+    out_rows = out.rearrange("(h p) g -> p h g", h=2)
     half = N // 2
     half_g = G // 2
 
@@ -35,7 +35,7 @@ def tile_attend_edge_uniq_bias_kernel(tc, xT, w, bias, offs, out):
         offsets = held.tile([P, N // 16], U16, name="offsets")
         raw = [held.tile([P, T], F32, name=f"raw_{t}", align_bytes=64) for t in range(PACK)]
         raw_w = held.tile([P, PACK, M], F32, name="raw_w", align_bytes=64)
-        bias_cols = held.tile([P, 2], F32, name="bias_cols")
+        bias_col = [held.tile([P, 1], F32, name=f"bias_col_{h}") for h in range(2)]
 
         nc.sync.dma_start(raw[2][:], x_rows[:, 2, :])
         nc.sync.dma_start(offsets[:], offs)
@@ -43,7 +43,8 @@ def tile_attend_edge_uniq_bias_kernel(tc, xT, w, bias, offs, out):
         nc.sync.dma_start(raw[3][:], x_rows[:, 3, :])
         nc.sync.dma_start(raw[1][:], x_rows[:, 1, :])
         nc.sync.dma_start(raw_w[:], w_rows)
-        nc.sync.dma_start(bias_cols[:], bias.rearrange("(p h) o -> p (h o)", h=2))
+        for h in range(2):
+            nc.sync.dma_start(bias_col[h][:], bias[P * h : P * h + P, :])
 
         cast_2 = held.tile([P, T], BF16, name="cast_2", align_bytes=64)
         cast_3 = held.tile([P, T], BF16, name="cast_3", align_bytes=64)
@@ -71,8 +72,14 @@ def tile_attend_edge_uniq_bias_kernel(tc, xT, w, bias, offs, out):
         nc.vector.tensor_copy(cast_3[:, CAST_SPLIT:T], raw[3][:, CAST_SPLIT:T])
         gather_s(3, cast_3, 0, ENTRY_SPLIT)
         gather_v(3, ENTRY_SPLIT, N)
-        for h in range(2):
-            nc.scalar.activation(w_grouped[:, h, :, :], raw_w[:].rearrange("p t (m h) -> p h m t", h=2)[:, h, :, :], COPY)
+        def w_views(lo, hi):
+            dst = w_flat[:, lo:hi, :].rearrange("p (c i) t -> p c t i", i=4)
+            src = raw_w[:, :, lo:hi].rearrange("p t (c i) -> p c t i", i=4)
+            return dst, src
+
+        w_flat = w_grouped[:].rearrange("p h m t -> p (h m) t")
+        nc.scalar.activation(*w_views(0, P), COPY)
+        nc.scalar.activation(*w_views(P, M), COPY)
         for i in range(2):
             gather_v(1, half * i, half * i + half)
         nc.vector.quantize_mx(x_codes[:, 0:half].bitcast(FP8X4), x_scales[:, 0:half], x_flat[:, 0 : 4 * half])
@@ -101,7 +108,7 @@ def tile_attend_edge_uniq_bias_kernel(tc, xT, w, bias, offs, out):
             nc.vector.tensor_reduce(top, acc[:].rearrange("p (g j) -> p g j", j=K), AXIS_X, MAX)
 
         def add_bias(res, top, h):
-            nc.scalar.activation(res, top, IDENTITY, bias=bias_cols[:, h : h + 1])
+            nc.scalar.activation(res, top, IDENTITY, bias=bias_col[h][:])
 
         acc_00 = multiply(0, 0, 256)
         acc_10 = multiply(1, 0, 256)

@@ -48,9 +48,9 @@ def tile_attend_edge_uniq_bias_kernel(tc, xT, w, bias, offs, out):
 
         cast_2 = held.tile([P, T], BF16, name="cast_2", align_bytes=64)
         cast_3 = held.tile([P, T], BF16, name="cast_3", align_bytes=64)
-        w_grouped = held.tile([P, 2, P, PACK], BF16, name="w_grouped", align_bytes=64)
+        w_grouped = [held.tile([P, P, PACK], BF16, name=f"w_grouped_{h}", tag=f"w_grouped_{h}", align_bytes=64) for h in range(2)]
         x_grouped = held.tile([P, N, PACK], BF16, name="x_grouped", align_bytes=64)
-        x_codes = held.tile([P, N], U32, name="x_codes", align_bytes=64)
+        x_codes = [held.tile([P, half], U32, name="x_codes_0", align_bytes=64)]
         x_scales = held.tile([P, N], U8, name="x_scales", align_bytes=64)
         w_codes = held.tile([P, M], U32, name="w_codes", align_bytes=64)
         w_scales = held.tile([P, M], U8, name="w_scales", align_bytes=64)
@@ -72,24 +72,34 @@ def tile_attend_edge_uniq_bias_kernel(tc, xT, w, bias, offs, out):
         nc.vector.tensor_copy(cast_3[:, CAST_SPLIT:T], raw[3][:, CAST_SPLIT:T])
         gather_s(3, cast_3, 0, ENTRY_SPLIT)
         gather_v(3, ENTRY_SPLIT, N)
-        def w_views(lo, hi):
-            dst = w_flat[:, lo:hi, :].rearrange("p (c i) t -> p c t i", i=4)
-            src = raw_w[:, :, lo:hi].rearrange("p t (c i) -> p c t i", i=4)
-            return dst, src
+        def cast_w(h):
+            dst = w_grouped[h][:].rearrange("p (c i) t -> p c t i", i=4)
+            src = raw_w[:, :, P * h : P * h + P].rearrange("p t (c i) -> p c t i", i=4)
+            nc.scalar.activation(dst, src, COPY)
 
-        w_flat = w_grouped[:].rearrange("p h m t -> p (h m) t")
-        nc.scalar.activation(*w_views(0, P), COPY)
-        nc.scalar.activation(*w_views(P, M), COPY)
-        for i in range(2):
-            gather_v(1, half * i, half * i + half)
-        nc.vector.quantize_mx(x_codes[:, 0:half].bitcast(FP8X4), x_scales[:, 0:half], x_flat[:, 0 : 4 * half])
-        for h in range(2):
+        def quantize_w(h):
             nc.vector.quantize_mx(
                 w_codes[:, P * h : P * h + P].bitcast(FP8X4),
                 w_scales[:, P * h : P * h + P],
-                w_grouped[:, h, :, :].rearrange("p m t -> p (m t)"),
+                w_grouped[h][:].rearrange("p m t -> p (m t)"),
             )
-        nc.vector.quantize_mx(x_codes[:, half:N].bitcast(FP8X4), x_scales[:, half:N], x_flat[:, 4 * half : 4 * N])
+
+        def quantize_x(i):
+            nc.vector.quantize_mx(
+                x_codes[i][:].bitcast(FP8X4),
+                x_scales[:, half * i : half * i + half],
+                x_flat[:, PACK * half * i : PACK * half * (i + 1)],
+            )
+
+        for h in range(2):
+            cast_w(h)
+        for i in range(2):
+            gather_v(1, half * i, half * i + half)
+        quantize_x(0)
+        quantize_w(0)
+        x_codes.append(held.tile([P, half], U32, name="x_codes_1", tag="w_grouped_0", align_bytes=64))
+        quantize_x(1)
+        quantize_w(1)
 
         def multiply(h, lo, hi):
             acc = psum.tile([P, hi - lo], F32, name=f"acc_{h}_{lo}")
@@ -97,7 +107,7 @@ def tile_attend_edge_uniq_bias_kernel(tc, xT, w, bias, offs, out):
                 out=acc[:],
                 lhsT=w_codes[:, P * h : P * h + P].bitcast(FP8X4),
                 lhsT_scale=w_scales[:, P * h : P * h + P],
-                rhs=x_codes[:, lo:hi].bitcast(FP8X4),
+                rhs=x_codes[lo // half][:, lo % half : lo % half + hi - lo].bitcast(FP8X4),
                 rhs_scale=x_scales[:, lo:hi],
                 start=True,
                 stop=True,

@@ -121,26 +121,20 @@ def tile_attend_edge_uniq_bias_kernel(tc, xT, w, bias, offs, out):
             nc.scalar.activation(res, top, IDENTITY, bias=bias_col[h][:])
 
         acc_00 = multiply(0, 0, 256)
-        acc_10 = multiply(1, 0, 256)
         acc_01 = multiply(0, 256, 512)
+        acc_10 = multiply(1, 0, 256)
         acc_11 = multiply(1, 256, 384)
         acc_12 = multiply(1, 384, 512)
-        tops = []
-        ress = []
-        for i in range(2):
-            top = held.tile([P, 2, half_g], F32, name=f"top_{i}")
-            res = held.tile([P, 2, half_g], F32, name=f"res_{i}")
-            tops.append(top)
-            ress.append(res)
-        largest(tops[0][:, 0, :], acc_00)
-        add_bias(ress[0][:, 0, :], tops[0][:, 0, :], 0)
-        largest(tops[0][:, 1, :], acc_10)
-        add_bias(ress[0][:, 1, :], tops[0][:, 1, :], 1)
-        nc.sync.dma_start(out_rows[:, :, 0:half_g], ress[0][:])
-        largest(tops[1][:, 0, :], acc_01)
-        add_bias(ress[1][:, 0, :], tops[1][:, 0, :], 0)
-        nc.sync.dma_start(out_rows[:, 0, half_g:G], ress[1][:, 0, :])
-        largest(tops[1][:, 1, 0:32], acc_11)
-        largest(tops[1][:, 1, 32:64], acc_12)
-        add_bias(ress[1][:, 1, :], tops[1][:, 1, :], 1)
-        nc.sync.dma_start(out_rows[:, 1, half_g:G], ress[1][:, 1, :])
+        res = [held.tile([P, G], F32, name=f"res_{h}") for h in range(2)]
+        top = [held.tile([P, G], F32, name=f"top_{h}") for h in range(2)]
+        largest(top[0][:, 0:half_g], acc_00)
+        largest(top[0][:, half_g:G], acc_01)
+        add_bias(res[0][:], top[0][:], 0)
+        nc.sync.dma_start(out_rows[:, 0, :], res[0][:])
+        largest(top[1][:, 0:half_g], acc_10)
+        largest(top[1][:, 64:96], acc_11)
+        add_bias(res[1][:, 0:96], top[1][:, 0:96], 1)
+        nc.sync.dma_start(out_rows[:, 1, 0:96], res[1][:, 0:96])
+        largest(top[1][:, 96:128], acc_12)
+        add_bias(res[1][:, 96:G], top[1][:, 96:G], 1)
+        nc.sync.dma_start(out_rows[:, 1, 96:G], res[1][:, 96:G])

@@ -17,7 +17,7 @@ G, K, T, D, M = 128, 4, 1024, 512, 256
 N = G * K
 FLOPS = 2 * D * M * N
 CAST_SPLIT = 640
-ENTRY_SPLIT = 352
+ENTRY_SPLIT = 384
 
 
 def tile_attend_edge_uniq_bias_kernel(tc, xT, w, bias, offs, out):
@@ -48,14 +48,11 @@ def tile_attend_edge_uniq_bias_kernel(tc, xT, w, bias, offs, out):
 
         cast_2 = held.tile([P, T], BF16, name="cast_2", align_bytes=64)
         cast_3 = held.tile([P, T], BF16, name="cast_3", align_bytes=64)
-        w_grouped = [held.tile([P, P, PACK], BF16, name=f"w_grouped_{h}", tag=f"w_grouped_{h}", align_bytes=64) for h in range(2)]
-        x_grouped = held.tile([P, N, PACK], BF16, name="x_grouped", align_bytes=64)
-        x_codes = [held.tile([P, half], U32, name="x_codes_0", align_bytes=64)]
-        x_scales = held.tile([P, N], U8, name="x_scales", align_bytes=64)
-        w_codes = held.tile([P, M], U32, name="w_codes", align_bytes=64)
-        w_scales = held.tile([P, M], U8, name="w_scales", align_bytes=64)
-
-        x_flat = x_grouped[:].rearrange("p c t -> p (c t)")
+        grouped = held.tile([P, P + N + P, PACK], BF16, name="grouped", align_bytes=64)
+        codes = held.tile([P, P + N + P], U32, name="codes", align_bytes=64)
+        scales = held.tile([P, P + N + P], U8, name="scales", align_bytes=64)
+        x_grouped = grouped[:, P : P + N, :]
+        w_at = (0, P + N)
 
         def gather_v(t, lo, hi):
             nc.vector.tensor_copy(x_grouped[:, lo:hi, t], raw[t][:].indirect(offsets[:, lo // 16 : hi // 16]))
@@ -72,69 +69,64 @@ def tile_attend_edge_uniq_bias_kernel(tc, xT, w, bias, offs, out):
         nc.vector.tensor_copy(cast_3[:, CAST_SPLIT:T], raw[3][:, CAST_SPLIT:T])
         gather_s(3, cast_3, 0, ENTRY_SPLIT)
         gather_v(3, ENTRY_SPLIT, N)
+
         def cast_w(h):
-            dst = w_grouped[h][:].rearrange("p (c i) t -> p c t i", i=4)
+            dst = grouped[:, w_at[h] : w_at[h] + P, :].rearrange("p (c i) t -> p c t i", i=4)
             src = raw_w[:, :, P * h : P * h + P].rearrange("p t (c i) -> p c t i", i=4)
             nc.scalar.activation(dst, src, COPY)
 
-        def quantize_w(h):
+        def quantize(lo, hi):
             nc.vector.quantize_mx(
-                w_codes[:, P * h : P * h + P].bitcast(FP8X4),
-                w_scales[:, P * h : P * h + P],
-                w_grouped[h][:].rearrange("p m t -> p (m t)"),
-            )
-
-        def quantize_x(i):
-            nc.vector.quantize_mx(
-                x_codes[i][:].bitcast(FP8X4),
-                x_scales[:, half * i : half * i + half],
-                x_flat[:, PACK * half * i : PACK * half * (i + 1)],
+                codes[:, lo:hi].bitcast(FP8X4),
+                scales[:, lo:hi],
+                grouped[:, lo:hi, :].rearrange("p c t -> p (c t)"),
             )
 
         for h in range(2):
             cast_w(h)
-        for i in range(2):
-            gather_v(1, half * i, half * i + half)
-        quantize_x(0)
-        quantize_w(0)
-        x_codes.append(held.tile([P, half], U32, name="x_codes_1", tag="w_grouped_0", align_bytes=64))
-        quantize_x(1)
-        quantize_w(1)
+        gather_v(1, 128, 384)
+        gather_v(1, 0, 128)
+        gather_v(1, 384, 512)
+        quantize(256, 512)
+        quantize(0, 256)
+        quantize(512, 768)
 
-        def multiply(h, lo, hi):
-            acc = psum.tile([P, hi - lo], F32, name=f"acc_{h}_{lo}")
+        def multiply(acc, h, lo, hi):
             nc.tensor.matmul_mx(
-                out=acc[:],
-                lhsT=w_codes[:, P * h : P * h + P].bitcast(FP8X4),
-                lhsT_scale=w_scales[:, P * h : P * h + P],
-                rhs=x_codes[lo // half][:, lo % half : lo % half + hi - lo].bitcast(FP8X4),
-                rhs_scale=x_scales[:, lo:hi],
+                out=acc,
+                lhsT=codes[:, w_at[h] : w_at[h] + P].bitcast(FP8X4),
+                lhsT_scale=scales[:, w_at[h] : w_at[h] + P],
+                rhs=codes[:, P + lo : P + hi].bitcast(FP8X4),
+                rhs_scale=scales[:, P + lo : P + hi],
                 start=True,
                 stop=True,
             )
-            return acc
 
         def largest(top, acc):
-            nc.vector.tensor_reduce(top, acc[:].rearrange("p (g j) -> p g j", j=K), AXIS_X, MAX)
+            nc.vector.tensor_reduce(top, acc.rearrange("p (g j) -> p g j", j=K), AXIS_X, MAX)
 
         def add_bias(res, top, h):
             nc.scalar.activation(res, top, IDENTITY, bias=bias_col[h][:])
 
-        acc_00 = multiply(0, 0, 256)
-        acc_01 = multiply(0, 256, 512)
-        acc_10 = multiply(1, 0, 256)
-        acc_11 = multiply(1, 256, 384)
-        acc_12 = multiply(1, 384, 512)
         res = [held.tile([P, G], F32, name=f"res_{h}") for h in range(2)]
         top = [held.tile([P, G], F32, name=f"top_{h}") for h in range(2)]
-        largest(top[0][:, 0:half_g], acc_00)
-        largest(top[0][:, half_g:G], acc_01)
-        add_bias(res[0][:], top[0][:], 0)
-        nc.sync.dma_start(out_rows[:, 0, :], res[0][:])
-        largest(top[1][:, 0:half_g], acc_10)
-        largest(top[1][:, 64:96], acc_11)
-        add_bias(res[1][:, 0:96], top[1][:, 0:96], 1)
-        nc.sync.dma_start(out_rows[:, 1, 0:96], res[1][:, 0:96])
-        largest(top[1][:, 96:128], acc_12)
-        add_bias(res[1][:, 96:G], top[1][:, 96:G], 1)
-        nc.sync.dma_start(out_rows[:, 1, 96:G], res[1][:, 96:G])
+
+        def nodes(h, *cuts):
+            lo, hi = cuts[0], cuts[-1]
+            acc = psum.tile([P, K * (hi - lo)], F32, name=f"acc_{h}_{lo}")
+            for a, b in zip(cuts, cuts[1:]):
+                multiply(acc[:, K * (a - lo) : K * (b - lo)], h, K * a, K * b)
+            largest(top[h][:, lo:hi], acc[:])
+
+        def leave(h, lo, hi):
+            add_bias(res[h][:, lo:hi], top[h][:, lo:hi], h)
+            nc.sync.dma_start(out_rows[:, h, lo:hi], res[h][:, lo:hi])
+
+        nodes(0, 0, 64)
+        nodes(0, 64, 96, 128)
+        leave(0, 0, G)
+        nodes(1, 0, 64)
+        leave(1, 0, 64)
+        nodes(1, 64, 96)
+        nodes(1, 96, 128)
+        leave(1, 64, G)

@@ -2,6 +2,7 @@ import concourse.mybir as mybir
 
 F32 = mybir.dt.float32
 BF16 = mybir.dt.bfloat16
+I32 = mybir.dt.int32
 U32 = mybir.dt.uint32
 U16 = mybir.dt.uint16
 U8 = mybir.dt.uint8
@@ -9,6 +10,7 @@ FP8X4 = mybir.dt.float8_e4m3fn_x4
 COPY = mybir.ActivationFunctionType.Copy
 IDENTITY = mybir.ActivationFunctionType.Identity
 MAX = mybir.AluOpType.max
+ADD = mybir.AluOpType.add
 AXIS_X = mybir.AxisListType.X
 
 P = 128
@@ -16,8 +18,9 @@ PACK = 4
 G, K, T, D, M = 128, 4, 1024, 512, 256
 N = G * K
 FLOPS = 2 * D * M * N
-CAST_SPLIT = 640
-ENTRY_SPLIT = 384
+CHUNK = 128
+CHUNKS = N // CHUNK
+SCALAR_FROM = 2
 
 
 def tile_attend_edge_uniq_bias_kernel(tc, xT, w, bias, offs, out):
@@ -26,7 +29,6 @@ def tile_attend_edge_uniq_bias_kernel(tc, xT, w, bias, offs, out):
     w_rows = w.rearrange("(p t) m -> p t m", t=PACK)
     out_rows = out.rearrange("(h p) g -> p h g", h=2)
     half = N // 2
-    half_g = G // 2
 
     with (
         tc.tile_pool(name="held", bufs=1) as held,
@@ -39,91 +41,88 @@ def tile_attend_edge_uniq_bias_kernel(tc, xT, w, bias, offs, out):
 
         nc.sync.dma_start(raw[2][:], x_rows[:, 2, :])
         nc.sync.dma_start(offsets[:], offs)
-        nc.sync.dma_start(raw[0][:], x_rows[:, 0, :])
-        nc.sync.dma_start(raw[3][:], x_rows[:, 3, :])
-        nc.sync.dma_start(raw[1][:], x_rows[:, 1, :])
+        for t in (3, 0, 1):
+            nc.sync.dma_start(raw[t][:], x_rows[:, t, :])
         nc.sync.dma_start(raw_w[:], w_rows)
         for h in range(2):
             nc.sync.dma_start(bias_col[h][:], bias[P * h : P * h + P, :])
 
-        cast_2 = held.tile([P, T], BF16, name="cast_2", align_bytes=64)
-        cast_3 = held.tile([P, T], BF16, name="cast_3", align_bytes=64)
-        grouped = held.tile([P, P + N + P, PACK], BF16, name="grouped", align_bytes=64)
-        codes = held.tile([P, P + N + P], U32, name="codes", align_bytes=64)
-        scales = held.tile([P, P + N + P], U8, name="scales", align_bytes=64)
-        x_grouped = grouped[:, P : P + N, :]
-        w_at = (0, P + N)
+        cast = {t: held.tile([P, T], BF16, name=f"cast_{t}", align_bytes=64) for t in (2, 3)}
+        pairs = held.tile([P, CHUNKS, 2, CHUNK, 2], BF16, name="pairs", align_bytes=64)
+        x_grouped = [held.tile([P, half, PACK], BF16, name=f"x_grouped_{s}", align_bytes=64) for s in range(2)]
+        w_grouped = [held.tile([P, P, PACK], BF16, name=f"w_grouped_{h}", align_bytes=64) for h in range(2)]
+        x_codes = [held.tile([P, half], U32, name=f"x_codes_{s}", align_bytes=64) for s in range(2)]
+        x_scales = [held.tile([P, half], U8, name=f"x_scales_{s}", align_bytes=64) for s in range(2)]
+        w_codes = [held.tile([P, P], U32, name=f"w_codes_{h}", align_bytes=64) for h in range(2)]
+        w_scales = [held.tile([P, P], U8, name=f"w_scales_{h}", align_bytes=64) for h in range(2)]
+
+        def listed(lo, hi):
+            return offsets[:, CHUNK * lo // 16 : CHUNK * hi // 16]
 
         def gather_v(t, lo, hi):
-            nc.vector.tensor_copy(x_grouped[:, lo:hi, t], raw[t][:].indirect(offsets[:, lo // 16 : hi // 16]))
+            nc.vector.tensor_copy(pairs[:, lo:hi, t // 2, :, t % 2], raw[t][:].indirect(listed(lo, hi)))
 
-        def gather_s(t, cast, lo, hi):
-            nc.scalar.activation(x_grouped[:, lo:hi, t], cast[:].indirect(offsets[:, lo // 16 : hi // 16]), COPY)
+        def gather_s(t, lo, hi):
+            nc.scalar.activation(pairs[:, lo:hi, t // 2, :, t % 2], cast[t][:].indirect(listed(lo, hi)), COPY)
 
-        nc.scalar.activation(cast_2[:, 0:256], raw[2][:, 0:256], COPY)
-        nc.vector.tensor_copy(cast_2[:, 256:T], raw[2][:, 256:T])
-        gather_s(2, cast_2, 0, ENTRY_SPLIT)
-        gather_v(2, ENTRY_SPLIT, N)
-        gather_v(0, 0, N)
-        nc.scalar.activation(cast_3[:, 0:CAST_SPLIT], raw[3][:, 0:CAST_SPLIT], COPY)
-        nc.vector.tensor_copy(cast_3[:, CAST_SPLIT:T], raw[3][:, CAST_SPLIT:T])
-        gather_s(3, cast_3, 0, ENTRY_SPLIT)
-        gather_v(3, ENTRY_SPLIT, N)
+        def weave_views(c, word):
+            at = CHUNK * (c % 2)
+            dst = x_grouped[c // 2][:, at : at + CHUNK, :].rearrange("p c t -> p (c t)").bitcast(word)
+            src = pairs[:, c].rearrange("p u c e -> p (u c e)").bitcast(word)
+            return dst.rearrange("p (c u) -> p c u", u=2), src.rearrange("p (u c) -> p c u", u=2)
 
-        def cast_w(h):
-            dst = grouped[:, w_at[h] : w_at[h] + P, :].rearrange("p (c i) t -> p c t i", i=4)
+        def w_views(h):
+            dst = w_grouped[h][:].rearrange("p (c i) t -> p c t i", i=4)
             src = raw_w[:, :, P * h : P * h + P].rearrange("p t (c i) -> p c t i", i=4)
-            nc.scalar.activation(dst, src, COPY)
+            return dst, src
 
-        def quantize(lo, hi):
-            nc.vector.quantize_mx(
-                codes[:, lo:hi].bitcast(FP8X4),
-                scales[:, lo:hi],
-                grouped[:, lo:hi, :].rearrange("p c t -> p (c t)"),
-            )
+        def quantize(codes, scales, grouped):
+            nc.vector.quantize_mx(codes[:].bitcast(FP8X4), scales[:], grouped[:].rearrange("p c t -> p (c t)"))
 
-        for h in range(2):
-            cast_w(h)
-        gather_v(1, 128, 384)
-        gather_v(1, 0, 128)
-        gather_v(1, 384, 512)
-        quantize(256, 512)
-        quantize(0, 256)
-        quantize(512, 768)
+        for t in (2, 3):
+            nc.scalar.activation(cast[t][:], raw[t][:], COPY)
+            gather_s(t, SCALAR_FROM, CHUNKS)
+            gather_v(t, 0, SCALAR_FROM)
+        gather_v(0, 0, CHUNKS)
+        for lo, hi in ((0, 1), (2, 3), (1, 2), (3, 4)):
+            gather_v(1, lo, hi)
+        nc.scalar.copy(*weave_views(0, U32))
+        nc.scalar.copy(*weave_views(2, U32))
+        nc.scalar.copy(*weave_views(1, U32))
+        nc.scalar.copy(*weave_views(3, U32))
+        nc.vector.tensor_copy(*w_views(0))
+
+        nc.scalar.activation(*w_views(1), COPY)
+        for s in range(2):
+            quantize(x_codes[s], x_scales[s], x_grouped[s])
+            quantize(w_codes[s], w_scales[s], w_grouped[s])
 
         def multiply(acc, h, lo, hi):
+            s, at = lo // half, lo % half
             nc.tensor.matmul_mx(
                 out=acc,
-                lhsT=codes[:, w_at[h] : w_at[h] + P].bitcast(FP8X4),
-                lhsT_scale=scales[:, w_at[h] : w_at[h] + P],
-                rhs=codes[:, P + lo : P + hi].bitcast(FP8X4),
-                rhs_scale=scales[:, P + lo : P + hi],
+                lhsT=w_codes[h][:].bitcast(FP8X4),
+                lhsT_scale=w_scales[h][:],
+                rhs=x_codes[s][:, at : at + hi - lo].bitcast(FP8X4),
+                rhs_scale=x_scales[s][:, at : at + hi - lo],
                 start=True,
                 stop=True,
             )
 
-        def largest(top, acc):
-            nc.vector.tensor_reduce(top, acc.rearrange("p (g j) -> p g j", j=K), AXIS_X, MAX)
-
-        def add_bias(res, top, h):
-            nc.scalar.activation(res, top, IDENTITY, bias=bias_col[h][:])
-
         res = [held.tile([P, G], F32, name=f"res_{h}") for h in range(2)]
         top = [held.tile([P, G], F32, name=f"top_{h}") for h in range(2)]
 
-        def nodes(h, *cuts):
-            lo, hi = cuts[0], cuts[-1]
+        def nodes(h, lo, hi):
             acc = psum.tile([P, K * (hi - lo)], F32, name=f"acc_{h}_{lo}")
-            for a, b in zip(cuts, cuts[1:]):
-                multiply(acc[:, K * (a - lo) : K * (b - lo)], h, K * a, K * b)
-            largest(top[h][:, lo:hi], acc[:])
+            multiply(acc[:], h, K * lo, K * hi)
+            nc.vector.tensor_reduce(top[h][:, lo:hi], acc[:].rearrange("p (g j) -> p g j", j=K), AXIS_X, MAX)
 
         def leave(h, lo, hi):
-            add_bias(res[h][:, lo:hi], top[h][:, lo:hi], h)
+            nc.scalar.activation(res[h][:, lo:hi], top[h][:, lo:hi], IDENTITY, bias=bias_col[h][:])
             nc.sync.dma_start(out_rows[:, h, lo:hi], res[h][:, lo:hi])
 
         nodes(0, 0, 64)
-        nodes(0, 64, 96, 128)
+        nodes(0, 64, 128)
         leave(0, 0, G)
         nodes(1, 0, 64)
         leave(1, 0, 64)

@@ -20,7 +20,6 @@ N = G * K
 FLOPS = 2 * D * M * N
 CHUNK = 128
 CHUNKS = N // CHUNK
-SCALAR_FROM = 2
 
 
 def tile_attend_edge_uniq_bias_kernel(tc, xT, w, bias, offs, out):
@@ -35,13 +34,14 @@ def tile_attend_edge_uniq_bias_kernel(tc, xT, w, bias, offs, out):
         tc.psum_pool(name="psum", bufs=1) as psum,
     ):
         offsets = held.tile([P, N // 16], U16, name="offsets")
-        raw = [held.tile([P, T], F32, name=f"raw_{t}", align_bytes=64) for t in range(PACK)]
+        raw_high = held.tile([P, 2, T], F32, name="raw_high", align_bytes=64)
+        raw = [held.tile([P, T], F32, name=f"raw_{t}", align_bytes=64) for t in range(2)]
         raw_w = held.tile([P, PACK, M], F32, name="raw_w", align_bytes=64)
         bias_col = [held.tile([P, 1], F32, name=f"bias_col_{h}") for h in range(2)]
 
-        nc.sync.dma_start(raw[2][:], x_rows[:, 2, :])
+        nc.sync.dma_start(raw_high[:], x_rows[:, 2:4, :])
         nc.sync.dma_start(offsets[:], offs)
-        for t in (3, 0, 1):
+        for t in range(2):
             nc.sync.dma_start(raw[t][:], x_rows[:, t, :])
         nc.sync.dma_start(raw_w[:], w_rows)
         for h in range(2):
@@ -79,10 +79,11 @@ def tile_attend_edge_uniq_bias_kernel(tc, xT, w, bias, offs, out):
         def quantize(codes, scales, grouped):
             nc.vector.quantize_mx(codes[:].bitcast(FP8X4), scales[:], grouped[:].rearrange("p c t -> p (c t)"))
 
+        nc.scalar.activation(cast[2][:], raw_high[:, 0, :], COPY)
+        nc.vector.tensor_copy(cast[3][:], raw_high[:, 1, :])
         for t in (2, 3):
-            nc.scalar.activation(cast[t][:], raw[t][:], COPY)
-            gather_s(t, SCALAR_FROM, CHUNKS)
-            gather_v(t, 0, SCALAR_FROM)
+            gather_s(t, 1, CHUNKS)
+            nc.vector.tensor_copy(pairs[:, 0, 1, :, t % 2], raw_high[:, t % 2, :].indirect(listed(0, 1)))
         gather_v(0, 0, CHUNKS)
         for lo, hi in ((0, 1), (2, 3), (1, 2), (3, 4)):
             gather_v(1, lo, hi)

@@ -2,7 +2,6 @@ import concourse.mybir as mybir
 
 F32 = mybir.dt.float32
 BF16 = mybir.dt.bfloat16
-I32 = mybir.dt.int32
 U32 = mybir.dt.uint32
 U16 = mybir.dt.uint16
 U8 = mybir.dt.uint8
@@ -10,7 +9,6 @@ FP8X4 = mybir.dt.float8_e4m3fn_x4
 COPY = mybir.ActivationFunctionType.Copy
 IDENTITY = mybir.ActivationFunctionType.Identity
 MAX = mybir.AluOpType.max
-ADD = mybir.AluOpType.add
 AXIS_X = mybir.AxisListType.X
 
 P = 128
@@ -34,24 +32,24 @@ def tile_attend_edge_uniq_bias_kernel(tc, xT, w, bias, offs, out):
         tc.psum_pool(name="psum", bufs=1) as psum,
     ):
         offsets = held.tile([P, N // 16], U16, name="offsets")
-        raw_high = held.tile([P, 2, T], F32, name="raw_high", align_bytes=64)
-        raw = [held.tile([P, T], F32, name=f"raw_{t}", align_bytes=64) for t in range(2)]
+        raw = [held.tile([P, T], F32, name=f"raw_{t}", align_bytes=64) for t in range(PACK)]
         raw_w = held.tile([P, PACK, M], F32, name="raw_w", align_bytes=64)
         bias_col = [held.tile([P, 1], F32, name=f"bias_col_{h}") for h in range(2)]
 
-        nc.sync.dma_start(raw_high[:], x_rows[:, 2:4, :])
+        nc.sync.dma_start(raw[0][:], x_rows[:, 0, :])
         nc.sync.dma_start(offsets[:], offs)
-        for t in range(2):
+        for t in range(1, PACK):
             nc.sync.dma_start(raw[t][:], x_rows[:, t, :])
         nc.sync.dma_start(raw_w[:], w_rows)
         for h in range(2):
             nc.sync.dma_start(bias_col[h][:], bias[P * h : P * h + P, :])
 
-        cast = {t: held.tile([P, T], BF16, name=f"cast_{t}", align_bytes=64) for t in (2, 3)}
-        pairs = held.tile([P, CHUNKS, 2, CHUNK, 2], BF16, name="pairs", align_bytes=64)
-        x_grouped = [held.tile([P, half, PACK], BF16, name=f"x_grouped_{s}", align_bytes=64) for s in range(2)]
+        flat = held.tile([P, PACK, CHUNK], BF16, name="flat", align_bytes=64)
+        pairs = held.tile([P, 2, 2, CHUNK, 2], BF16, name="pairs", align_bytes=64)
+        x_direct = held.tile([P, CHUNK, PACK], BF16, name="x_direct", align_bytes=64)
+        x_second = held.tile([P, CHUNK, PACK], BF16, name="x_second", tag="reused", align_bytes=64)
+        x_upper = held.tile([P, half, PACK], BF16, name="x_upper", align_bytes=64)
         w_grouped = [held.tile([P, P, PACK], BF16, name=f"w_grouped_{h}", align_bytes=64) for h in range(2)]
-        x_codes = [held.tile([P, half], U32, name=f"x_codes_{s}", align_bytes=64) for s in range(2)]
         x_scales = [held.tile([P, half], U8, name=f"x_scales_{s}", align_bytes=64) for s in range(2)]
         w_codes = [held.tile([P, P], U32, name=f"w_codes_{h}", align_bytes=64) for h in range(2)]
         w_scales = [held.tile([P, P], U8, name=f"w_scales_{h}", align_bytes=64) for h in range(2)]
@@ -59,44 +57,61 @@ def tile_attend_edge_uniq_bias_kernel(tc, xT, w, bias, offs, out):
         def listed(lo, hi):
             return offsets[:, CHUNK * lo // 16 : CHUNK * hi // 16]
 
-        def gather_v(t, lo, hi):
-            nc.vector.tensor_copy(pairs[:, lo:hi, t // 2, :, t % 2], raw[t][:].indirect(listed(lo, hi)))
+        def gather_pairs(t, lo, hi):
+            nc.vector.tensor_copy(pairs[:, lo - 1 : hi - 1, t // 2, :, t % 2], raw[t][:].indirect(listed(lo, hi)))
 
-        def gather_s(t, lo, hi):
-            nc.scalar.activation(pairs[:, lo:hi, t // 2, :, t % 2], cast[t][:].indirect(listed(lo, hi)), COPY)
+        def gather_direct(t):
+            nc.vector.tensor_copy(x_direct[:, :, t], raw[t][:].indirect(listed(0, 1)))
 
-        def weave_views(c, word):
-            at = CHUNK * (c % 2)
-            dst = x_grouped[c // 2][:, at : at + CHUNK, :].rearrange("p c t -> p (c t)").bitcast(word)
-            src = pairs[:, c].rearrange("p u c e -> p (u c e)").bitcast(word)
-            return dst.rearrange("p (c u) -> p c u", u=2), src.rearrange("p (u c) -> p c u", u=2)
+        def gather_flat(t):
+            nc.scalar.activation(flat[:, t, :], raw[t][:].indirect(listed(3, 4)), COPY)
+
+        def place(u):
+            nc.scalar.copy(
+                x_upper[:, CHUNK:, 2 * u : 2 * u + 2],
+                flat[:, 2 * u : 2 * u + 2, :].rearrange("p e c -> p c e"),
+            )
+
+        def weave(c, values):
+            dst = values.rearrange("p c t -> p (c t)").bitcast(U32)
+            src = pairs[:, c - 1].rearrange("p u c e -> p (u c e)").bitcast(U32)
+            nc.scalar.copy(dst.rearrange("p (c u) -> p c u", u=2), src.rearrange("p (u c) -> p c u", u=2))
 
         def w_views(h):
             dst = w_grouped[h][:].rearrange("p (c i) t -> p c t i", i=4)
             src = raw_w[:, :, P * h : P * h + P].rearrange("p t (c i) -> p c t i", i=4)
             return dst, src
 
-        def quantize(codes, scales, grouped):
-            nc.vector.quantize_mx(codes[:].bitcast(FP8X4), scales[:], grouped[:].rearrange("p c t -> p (c t)"))
+        def quantize(codes, scales, values):
+            nc.vector.quantize_mx(codes.bitcast(FP8X4), scales, values.rearrange("p c t -> p (c t)"))
 
-        nc.scalar.activation(cast[2][:], raw_high[:, 0, :], COPY)
-        nc.vector.tensor_copy(cast[3][:], raw_high[:, 1, :])
-        for t in (2, 3):
-            gather_s(t, 1, CHUNKS)
-            nc.vector.tensor_copy(pairs[:, 0, 1, :, t % 2], raw_high[:, t % 2, :].indirect(listed(0, 1)))
-        gather_v(0, 0, CHUNKS)
-        for lo, hi in ((0, 1), (2, 3), (1, 2), (3, 4)):
-            gather_v(1, lo, hi)
-        nc.scalar.copy(*weave_views(0, U32))
-        nc.scalar.copy(*weave_views(2, U32))
-        nc.scalar.copy(*weave_views(1, U32))
-        nc.scalar.copy(*weave_views(3, U32))
+        warm = held.tile([P, 2], F32, name="warm")
+        nc.gpsimd.memset(warm[:, 0:1], 0.0)
+        nc.scalar.activation(warm[:, 1:2], warm[:, 0:1], COPY)
+
+        for t in range(PACK - 1):
+            gather_pairs(t, 1, 3)
+            gather_direct(t)
+            gather_flat(t)
+            if t == 1:
+                place(0)
+        gather_pairs(3, 2, 3)
+        gather_direct(3)
+        gather_pairs(3, 1, 2)
+        gather_flat(3)
+        weave(2, x_upper[:, :CHUNK, :])
+        place(1)
+        weave(1, x_second[:])
         nc.vector.tensor_copy(*w_views(0))
-
         nc.scalar.activation(*w_views(1), COPY)
-        for s in range(2):
-            quantize(x_codes[s], x_scales[s], x_grouped[s])
-            quantize(w_codes[s], w_scales[s], w_grouped[s])
+
+        x_codes = [held.tile([P, half], U32, name="x_codes_0", align_bytes=64)]
+        quantize(x_codes[0][:, :CHUNK], x_scales[0][:, :CHUNK], x_direct[:])
+        quantize(x_codes[0][:, CHUNK:], x_scales[0][:, CHUNK:], x_second[:])
+        quantize(w_codes[0][:], w_scales[0][:], w_grouped[0][:])
+        x_codes.append(held.tile([P, half], U32, name="x_codes_1", tag="reused", align_bytes=64))
+        quantize(x_codes[1][:], x_scales[1][:], x_upper[:])
+        quantize(w_codes[1][:], w_scales[1][:], w_grouped[1][:])
 
         def multiply(acc, h, lo, hi):
             s, at = lo // half, lo % half

@@ -46,13 +46,10 @@ def tile_attend_edge_uniq_bias_kernel(tc, xT, w, bias, offs, out):
 
         flat = held.tile([P, PACK, CHUNK], BF16, name="flat", align_bytes=64)
         pairs = held.tile([P, 2, 2, CHUNK, 2], BF16, name="pairs", align_bytes=64)
-        x_direct = held.tile([P, CHUNK, PACK], BF16, name="x_direct", align_bytes=64)
-        x_second = held.tile([P, CHUNK, PACK], BF16, name="x_second", tag="reused", align_bytes=64)
-        x_upper = held.tile([P, half, PACK], BF16, name="x_upper", align_bytes=64)
+        x_lower = held.tile([P, half, PACK], BF16, name="x_lower", align_bytes=64)
+        x_third = held.tile([P, CHUNK, PACK], BF16, name="x_third", tag="reused", align_bytes=64)
+        x_last = held.tile([P, CHUNK, PACK], BF16, name="x_last", align_bytes=64)
         w_grouped = [held.tile([P, P, PACK], BF16, name=f"w_grouped_{h}", align_bytes=64) for h in range(2)]
-        x_scales = [held.tile([P, half], U8, name=f"x_scales_{s}", align_bytes=64) for s in range(2)]
-        w_codes = [held.tile([P, P], U32, name=f"w_codes_{h}", align_bytes=64) for h in range(2)]
-        w_scales = [held.tile([P, P], U8, name=f"w_scales_{h}", align_bytes=64) for h in range(2)]
 
         def listed(lo, hi):
             return offsets[:, CHUNK * lo // 16 : CHUNK * hi // 16]
@@ -61,14 +58,14 @@ def tile_attend_edge_uniq_bias_kernel(tc, xT, w, bias, offs, out):
             nc.vector.tensor_copy(pairs[:, lo - 1 : hi - 1, t // 2, :, t % 2], raw[t][:].indirect(listed(lo, hi)))
 
         def gather_direct(t):
-            nc.vector.tensor_copy(x_direct[:, :, t], raw[t][:].indirect(listed(0, 1)))
+            nc.vector.tensor_copy(x_lower[:, :CHUNK, t], raw[t][:].indirect(listed(0, 1)))
 
         def gather_flat(t):
             nc.scalar.activation(flat[:, t, :], raw[t][:].indirect(listed(3, 4)), COPY)
 
         def place(u):
             nc.scalar.copy(
-                x_upper[:, CHUNK:, 2 * u : 2 * u + 2],
+                x_last[:, :, 2 * u : 2 * u + 2],
                 flat[:, 2 * u : 2 * u + 2, :].rearrange("p e c -> p c e"),
             )
 
@@ -82,8 +79,12 @@ def tile_attend_edge_uniq_bias_kernel(tc, xT, w, bias, offs, out):
             src = raw_w[:, :, P * h : P * h + P].rearrange("p t (c i) -> p c t i", i=4)
             return dst, src
 
-        def quantize(codes, scales, values):
-            nc.vector.quantize_mx(codes.bitcast(FP8X4), scales, values.rearrange("p c t -> p (c t)"))
+        def quantize(name, values, tag=None):
+            width = values.shape[1]
+            codes = held.tile([P, width], U32, name=f"{name}_codes", tag=tag or f"{name}_codes", align_bytes=64)
+            scales = held.tile([P, width], U8, name=f"{name}_scales", align_bytes=64)
+            nc.vector.quantize_mx(codes[:].bitcast(FP8X4), scales[:], values[:].rearrange("p c t -> p (c t)"))
+            return codes, scales
 
         warm = held.tile([P, 2], F32, name="warm")
         nc.gpsimd.memset(warm[:, 0:1], 0.0)
@@ -95,32 +96,29 @@ def tile_attend_edge_uniq_bias_kernel(tc, xT, w, bias, offs, out):
             gather_flat(t)
             if t == 1:
                 place(0)
-        gather_pairs(3, 2, 3)
-        gather_direct(3)
         gather_pairs(3, 1, 2)
+        gather_direct(3)
+        gather_pairs(3, 2, 3)
         gather_flat(3)
-        weave(2, x_upper[:, :CHUNK, :])
+        weave(1, x_lower[:, CHUNK:, :])
         place(1)
-        weave(1, x_second[:])
+        weave(2, x_third[:])
         nc.vector.tensor_copy(*w_views(0))
         nc.scalar.activation(*w_views(1), COPY)
 
-        x_codes = [held.tile([P, half], U32, name="x_codes_0", align_bytes=64)]
-        quantize(x_codes[0][:, :CHUNK], x_scales[0][:, :CHUNK], x_direct[:])
-        quantize(x_codes[0][:, CHUNK:], x_scales[0][:, CHUNK:], x_second[:])
-        quantize(w_codes[0][:], w_scales[0][:], w_grouped[0][:])
-        x_codes.append(held.tile([P, half], U32, name="x_codes_1", tag="reused", align_bytes=64))
-        quantize(x_codes[1][:], x_scales[1][:], x_upper[:])
-        quantize(w_codes[1][:], w_scales[1][:], w_grouped[1][:])
+        lower = quantize("lower", x_lower)
+        third = quantize("third", x_third)
+        weights = [quantize("w_0", w_grouped[0])]
+        last = quantize("last", x_last, tag="reused")
+        weights.append(quantize("w_1", w_grouped[1]))
 
-        def multiply(acc, h, lo, hi):
-            s, at = lo // half, lo % half
+        def multiply(acc, h, operand):
             nc.tensor.matmul_mx(
                 out=acc,
-                lhsT=w_codes[h][:].bitcast(FP8X4),
-                lhsT_scale=w_scales[h][:],
-                rhs=x_codes[s][:, at : at + hi - lo].bitcast(FP8X4),
-                rhs_scale=x_scales[s][:, at : at + hi - lo],
+                lhsT=weights[h][0][:].bitcast(FP8X4),
+                lhsT_scale=weights[h][1][:],
+                rhs=operand[0][:].bitcast(FP8X4),
+                rhs_scale=operand[1][:],
                 start=True,
                 stop=True,
             )
@@ -128,20 +126,23 @@ def tile_attend_edge_uniq_bias_kernel(tc, xT, w, bias, offs, out):
         res = [held.tile([P, G], F32, name=f"res_{h}") for h in range(2)]
         top = [held.tile([P, G], F32, name=f"top_{h}") for h in range(2)]
 
-        def nodes(h, lo, hi):
-            acc = psum.tile([P, K * (hi - lo)], F32, name=f"acc_{h}_{lo}")
-            multiply(acc[:], h, K * lo, K * hi)
+        def nodes(h, lo, operands):
+            widths = [operand[0].shape[1] for operand in operands]
+            acc = psum.tile([P, sum(widths)], F32, name=f"acc_{h}_{lo}")
+            for i, operand in enumerate(operands):
+                multiply(acc[:, sum(widths[:i]) : sum(widths[: i + 1])], h, operand)
+            hi = lo + sum(widths) // K
             nc.vector.tensor_reduce(top[h][:, lo:hi], acc[:].rearrange("p (g j) -> p g j", j=K), AXIS_X, MAX)
 
         def leave(h, lo, hi):
             nc.scalar.activation(res[h][:, lo:hi], top[h][:, lo:hi], IDENTITY, bias=bias_col[h][:])
             nc.sync.dma_start(out_rows[:, h, lo:hi], res[h][:, lo:hi])
 
-        nodes(0, 0, 64)
-        nodes(0, 64, 128)
+        nodes(0, 0, [lower])
+        nodes(0, 64, [third, last])
         leave(0, 0, G)
-        nodes(1, 0, 64)
+        nodes(1, 0, [lower])
         leave(1, 0, 64)
-        nodes(1, 64, 96)
-        nodes(1, 96, 128)
+        nodes(1, 64, [third])
+        nodes(1, 96, [last])
         leave(1, 64, G)

@@ -8,6 +8,8 @@ U8 = mybir.dt.uint8
 FP8X4 = mybir.dt.float8_e4m3fn_x4
 COPY = mybir.ActivationFunctionType.Copy
 IDENTITY = mybir.ActivationFunctionType.Identity
+MULT = mybir.AluOpType.mult
+ADD = mybir.AluOpType.add
 MAX = mybir.AluOpType.max
 AXIS_X = mybir.AxisListType.X
 
@@ -17,7 +19,8 @@ G, K, T, D, M = 128, 4, 1024, 512, 256
 N = G * K
 FLOPS = 2 * D * M * N
 CHUNK = 128
-CHUNKS = N // CHUNK
+GPSIMD_SHARE = 96
+VECTOR_SHARE = 32
 
 
 def tile_attend_edge_uniq_bias_kernel(tc, xT, w, bias, offs, out):
@@ -33,98 +36,115 @@ def tile_attend_edge_uniq_bias_kernel(tc, xT, w, bias, offs, out):
     ):
         offsets = held.tile([P, N // 16], U16, name="offsets")
         raw = [held.tile([P, T], F32, name=f"raw_{t}", align_bytes=64) for t in range(PACK)]
-        raw_w = held.tile([P, PACK, M], F32, name="raw_w", align_bytes=64)
+        raw_w = [
+            held.tile([P, PACK, P], F32, name="raw_w_0", tag="reused", align_bytes=64),
+            held.tile([P, PACK, P], F32, name="raw_w_1", align_bytes=64),
+        ]
         bias_col = [held.tile([P, 1], F32, name=f"bias_col_{h}") for h in range(2)]
 
         nc.sync.dma_start(raw[0][:], x_rows[:, 0, :])
         nc.sync.dma_start(offsets[:], offs)
         for t in range(1, PACK):
             nc.sync.dma_start(raw[t][:], x_rows[:, t, :])
-        nc.sync.dma_start(raw_w[:], w_rows)
+        for h in range(2):
+            nc.sync.dma_start(raw_w[h][:], w_rows[:, :, P * h : P * h + P])
         for h in range(2):
             nc.sync.dma_start(bias_col[h][:], bias[P * h : P * h + P, :])
 
         flat = held.tile([P, PACK, CHUNK], BF16, name="flat", align_bytes=64)
-        pairs = held.tile([P, 2, 2, CHUNK, 2], BF16, name="pairs", align_bytes=64)
-        x_lower = held.tile([P, half, PACK], BF16, name="x_lower", align_bytes=64)
-        x_third = held.tile([P, CHUNK, PACK], BF16, name="x_third", tag="reused", align_bytes=64)
-        x_last = held.tile([P, CHUNK, PACK], BF16, name="x_last", align_bytes=64)
-        w_grouped = [held.tile([P, P, PACK], BF16, name=f"w_grouped_{h}", align_bytes=64) for h in range(2)]
+        pairs = held.tile([P, 1, 2, CHUNK, 2], BF16, name="pairs", align_bytes=64)
+        x_all = held.tile([P, N, PACK], BF16, name="x_all", align_bytes=64)
+        x_lower, x_upper = x_all[:, :half, :], x_all[:, half:, :]
+        w_grouped = [
+            held.tile([P, P, PACK], BF16, name="w_grouped_0", align_bytes=64),
+            held.tile([P, P, PACK], BF16, name="w_grouped_1", tag="reused_late", align_bytes=64),
+        ]
 
         def listed(lo, hi):
             return offsets[:, CHUNK * lo // 16 : CHUNK * hi // 16]
 
         def gather_pairs(t, lo, hi):
-            nc.vector.tensor_copy(pairs[:, lo - 1 : hi - 1, t // 2, :, t % 2], raw[t][:].indirect(listed(lo, hi)))
+            nc.vector.tensor_copy(pairs[:, lo:hi, t // 2, :, t % 2], raw[t][:].indirect(listed(lo, hi)))
 
-        def gather_direct(t):
-            nc.vector.tensor_copy(x_lower[:, :CHUNK, t], raw[t][:].indirect(listed(0, 1)))
+        def weave(c):
+            dst = x_all[:, CHUNK * c : CHUNK * c + CHUNK, :].rearrange("p c t -> p (c t)").bitcast(U32)
+            src = pairs[:, c].rearrange("p u c e -> p (u c e)").bitcast(U32)
+            nc.scalar.copy(dst.rearrange("p (c u) -> p c u", u=2), src.rearrange("p (u c) -> p c u", u=2))
+
+        def gather_direct(t, lo, hi):
+            nc.vector.tensor_copy(x_all[:, CHUNK * lo : CHUNK * hi, t], raw[t][:].indirect(listed(lo, hi)))
 
         def gather_flat(t):
             nc.scalar.activation(flat[:, t, :], raw[t][:].indirect(listed(3, 4)), COPY)
 
         def place(u):
             nc.scalar.copy(
-                x_last[:, :, 2 * u : 2 * u + 2],
+                x_upper[:, CHUNK:, 2 * u : 2 * u + 2],
                 flat[:, 2 * u : 2 * u + 2, :].rearrange("p e c -> p c e"),
             )
 
-        def weave(c, values):
-            dst = values.rearrange("p c t -> p (c t)").bitcast(U32)
-            src = pairs[:, c - 1].rearrange("p u c e -> p (u c e)").bitcast(U32)
-            nc.scalar.copy(dst.rearrange("p (c u) -> p c u", u=2), src.rearrange("p (u c) -> p c u", u=2))
-
-        def w_views(h):
-            dst = w_grouped[h][:].rearrange("p (c i) t -> p c t i", i=4)
-            src = raw_w[:, :, P * h : P * h + P].rearrange("p t (c i) -> p c t i", i=4)
+        def w_views(h, lo, hi):
+            dst = w_grouped[h][:, lo:hi, :].rearrange("p (c i) t -> p c t i", i=4)
+            src = raw_w[h][:, :, lo:hi].rearrange("p t (c i) -> p c t i", i=4)
             return dst, src
 
         def quantize(name, values, tag=None):
             width = values.shape[1]
             codes = held.tile([P, width], U32, name=f"{name}_codes", tag=tag or f"{name}_codes", align_bytes=64)
             scales = held.tile([P, width], U8, name=f"{name}_scales", align_bytes=64)
-            nc.vector.quantize_mx(codes[:].bitcast(FP8X4), scales[:], values[:].rearrange("p c t -> p (c t)"))
-            return codes, scales
+            nc.vector.quantize_mx(codes[:].bitcast(FP8X4), scales[:], values.rearrange("p c t -> p (c t)"))
+            return codes[:], scales[:]
 
         warm = held.tile([P, 2], F32, name="warm")
         nc.gpsimd.memset(warm[:, 0:1], 0.0)
         nc.scalar.activation(warm[:, 1:2], warm[:, 0:1], COPY)
 
         for t in range(PACK - 1):
-            gather_pairs(t, 1, 3)
-            gather_direct(t)
+            gather_pairs(t, 0, 1)
+            gather_direct(t, 1, 3)
             gather_flat(t)
             if t == 1:
                 place(0)
-        gather_pairs(3, 1, 2)
-        gather_direct(3)
-        gather_pairs(3, 2, 3)
+        gather_pairs(3, 0, 1)
+        gather_direct(3, 1, 2)
+        gather_direct(3, 2, 3)
         gather_flat(3)
-        weave(1, x_lower[:, CHUNK:, :])
+        weave(0)
         place(1)
-        weave(2, x_third[:])
-        nc.vector.tensor_copy(*w_views(0))
-        nc.scalar.activation(*w_views(1), COPY)
+        nc.gpsimd.tensor_scalar(
+            w_grouped[0][:, :GPSIMD_SHARE, :],
+            raw_w[0][:, :, :GPSIMD_SHARE].rearrange("p t c -> p c t"),
+            1.0,
+            0.0,
+            op0=MULT,
+            op1=ADD,
+        )
+        nc.scalar.activation(*w_views(0, GPSIMD_SHARE, P), COPY)
+        nc.vector.tensor_copy(*w_views(1, 0, VECTOR_SHARE))
+        nc.scalar.activation(*w_views(1, VECTOR_SHARE, P), COPY)
 
         lower = quantize("lower", x_lower)
-        third = quantize("third", x_third)
-        weights = [quantize("w_0", w_grouped[0])]
-        last = quantize("last", x_last, tag="reused")
-        weights.append(quantize("w_1", w_grouped[1]))
+        weights = [quantize("w_0", w_grouped[0][:])]
+        upper = quantize("upper", x_upper, tag="reused")
+        weights.append(quantize("w_1", w_grouped[1][:]))
+        third, last = [[plane[:, at : at + CHUNK] for plane in upper] for at in (0, CHUNK)]
 
         def multiply(acc, h, operand):
             nc.tensor.matmul_mx(
                 out=acc,
-                lhsT=weights[h][0][:].bitcast(FP8X4),
-                lhsT_scale=weights[h][1][:],
-                rhs=operand[0][:].bitcast(FP8X4),
-                rhs_scale=operand[1][:],
+                lhsT=weights[h][0].bitcast(FP8X4),
+                lhsT_scale=weights[h][1],
+                rhs=operand[0].bitcast(FP8X4),
+                rhs_scale=operand[1],
                 start=True,
                 stop=True,
             )
 
-        res = [held.tile([P, G], F32, name=f"res_{h}") for h in range(2)]
-        top = [held.tile([P, G], F32, name=f"top_{h}") for h in range(2)]
+        res = held.tile([P, 2, G], F32, name="res")
+        top = [
+            held.tile([P, G], F32, name="top_0", tag="reused_late", align_bytes=64),
+            held.tile([P, G], F32, name="top_1", align_bytes=64),
+        ]
 
         def nodes(h, lo, operands):
             widths = [operand[0].shape[1] for operand in operands]
@@ -134,12 +154,15 @@ def tile_attend_edge_uniq_bias_kernel(tc, xT, w, bias, offs, out):
             hi = lo + sum(widths) // K
             nc.vector.tensor_reduce(top[h][:, lo:hi], acc[:].rearrange("p (g j) -> p g j", j=K), AXIS_X, MAX)
 
+        def add_bias(h, lo, hi):
+            nc.scalar.activation(res[:, h, lo:hi], top[h][:, lo:hi], IDENTITY, bias=bias_col[h][:])
+
         def leave(h, lo, hi):
-            nc.scalar.activation(res[h][:, lo:hi], top[h][:, lo:hi], IDENTITY, bias=bias_col[h][:])
-            nc.sync.dma_start(out_rows[:, h, lo:hi], res[h][:, lo:hi])
+            add_bias(h, lo, hi)
+            nc.sync.dma_start(out_rows[:, h, lo:hi], res[:, h, lo:hi])
 
         nodes(0, 0, [lower])
-        nodes(0, 64, [third, last])
+        nodes(0, 64, [upper])
         leave(0, 0, G)
         nodes(1, 0, [lower])
         leave(1, 0, 64)

@@ -95,10 +95,6 @@ def tile_attend_edge_uniq_bias_kernel(tc, xT, w, bias, offs, out):
             nc.vector.quantize_mx(codes[:].bitcast(FP8X4), scales[:], values.rearrange("p c t -> p (c t)"))
             return codes[:], scales[:]
 
-        warm = held.tile([P, 2], F32, name="warm")
-        nc.gpsimd.memset(warm[:, 0:1], 0.0)
-        nc.scalar.activation(warm[:, 1:2], warm[:, 0:1], COPY)
-
         for t in range(PACK - 1):
             gather_pairs(t, 0, 1)
             gather_direct(t, 1, 3)

@@ -8,8 +8,6 @@ U8 = mybir.dt.uint8
 FP8X4 = mybir.dt.float8_e4m3fn_x4
 COPY = mybir.ActivationFunctionType.Copy
 IDENTITY = mybir.ActivationFunctionType.Identity
-MULT = mybir.AluOpType.mult
-ADD = mybir.AluOpType.add
 MAX = mybir.AluOpType.max
 AXIS_X = mybir.AxisListType.X
 
@@ -19,8 +17,6 @@ G, K, T, D, M = 128, 4, 1024, 512, 256
 N = G * K
 FLOPS = 2 * D * M * N
 CHUNK = 128
-GPSIMD_SHARE = 96
-VECTOR_SHARE = 32
 
 
 def tile_attend_edge_uniq_bias_kernel(tc, xT, w, bias, offs, out):
@@ -51,7 +47,7 @@ def tile_attend_edge_uniq_bias_kernel(tc, xT, w, bias, offs, out):
         for h in range(2):
             nc.sync.dma_start(bias_col[h][:], bias[P * h : P * h + P, :])
 
-        flat = held.tile([P, PACK, CHUNK], BF16, name="flat", align_bytes=64)
+        flat = held.tile([P, PACK, CHUNK], BF16, name="flat", tag="rows", align_bytes=64)
         pairs = held.tile([P, 1, 2, CHUNK, 2], BF16, name="pairs", align_bytes=64)
         x_all = held.tile([P, N, PACK], BF16, name="x_all", align_bytes=64)
         x_lower, x_upper = x_all[:, :half, :], x_all[:, half:, :]
@@ -83,9 +79,9 @@ def tile_attend_edge_uniq_bias_kernel(tc, xT, w, bias, offs, out):
                 flat[:, 2 * u : 2 * u + 2, :].rearrange("p e c -> p c e"),
             )
 
-        def w_views(h, lo, hi):
-            dst = w_grouped[h][:, lo:hi, :].rearrange("p (c i) t -> p c t i", i=4)
-            src = raw_w[h][:, :, lo:hi].rearrange("p t (c i) -> p c t i", i=4)
+        def w_views(h):
+            dst = w_grouped[h][:].rearrange("p (c i) t -> p c t i", i=4)
+            src = raw_w[h][:].rearrange("p t (c i) -> p c t i", i=4)
             return dst, src
 
         def quantize(name, values, tag=None):
@@ -107,19 +103,10 @@ def tile_attend_edge_uniq_bias_kernel(tc, xT, w, bias, offs, out):
         gather_flat(3)
         weave(0)
         place(1)
-        nc.gpsimd.tensor_scalar(
-            w_grouped[0][:, :GPSIMD_SHARE, :],
-            raw_w[0][:, :, :GPSIMD_SHARE].rearrange("p t c -> p c t"),
-            1.0,
-            0.0,
-            op0=MULT,
-            op1=ADD,
-        )
-        nc.scalar.activation(*w_views(0, GPSIMD_SHARE, P), COPY)
-        nc.vector.tensor_copy(*w_views(1, 0, VECTOR_SHARE))
-        nc.scalar.activation(*w_views(1, VECTOR_SHARE, P), COPY)
+        nc.vector.tensor_copy(*w_views(0))
+        nc.scalar.activation(*w_views(1), COPY)
 
-        lower = quantize("lower", x_lower)
+        lower = quantize("lower", x_lower, tag="rows")
         weights = [quantize("w_0", w_grouped[0][:])]
         upper = quantize("upper", x_upper, tag="reused")
         weights.append(quantize("w_1", w_grouped[1][:]))

@@ -8,6 +8,8 @@ U8 = mybir.dt.uint8
 FP8X4 = mybir.dt.float8_e4m3fn_x4
 COPY = mybir.ActivationFunctionType.Copy
 IDENTITY = mybir.ActivationFunctionType.Identity
+MULT = mybir.AluOpType.mult
+ADD = mybir.AluOpType.add
 MAX = mybir.AluOpType.max
 AXIS_X = mybir.AxisListType.X
 
@@ -24,7 +26,6 @@ def tile_attend_edge_uniq_bias_kernel(tc, xT, w, bias, offs, out):
     x_rows = xT.rearrange("(p t) c -> p t c", t=PACK)
     w_rows = w.rearrange("(p t) m -> p t m", t=PACK)
     out_rows = out.rearrange("(h p) g -> p h g", h=2)
-    half = N // 2
 
     with (
         tc.tile_pool(name="held", bufs=1) as held,
@@ -34,7 +35,7 @@ def tile_attend_edge_uniq_bias_kernel(tc, xT, w, bias, offs, out):
         raw = [held.tile([P, T], F32, name=f"raw_{t}", align_bytes=64) for t in range(PACK)]
         raw_w = [
             held.tile([P, PACK, P], F32, name="raw_w_0", tag="reused", align_bytes=64),
-            held.tile([P, PACK, P], F32, name="raw_w_1", align_bytes=64),
+            held.tile([P, PACK, P], F32, name="raw_w_1", tag="reused_late", align_bytes=64),
         ]
         bias_col = [held.tile([P, 1], F32, name=f"bias_col_{h}") for h in range(2)]
 
@@ -47,14 +48,10 @@ def tile_attend_edge_uniq_bias_kernel(tc, xT, w, bias, offs, out):
         for h in range(2):
             nc.sync.dma_start(bias_col[h][:], bias[P * h : P * h + P, :])
 
-        flat = held.tile([P, PACK, CHUNK], BF16, name="flat", tag="rows", align_bytes=64)
+        flat = held.tile([P, PACK, CHUNK], BF16, name="flat", align_bytes=64)
         pairs = held.tile([P, 1, 2, CHUNK, 2], BF16, name="pairs", align_bytes=64)
         x_all = held.tile([P, N, PACK], BF16, name="x_all", align_bytes=64)
-        x_lower, x_upper = x_all[:, :half, :], x_all[:, half:, :]
-        w_grouped = [
-            held.tile([P, P, PACK], BF16, name="w_grouped_0", align_bytes=64),
-            held.tile([P, P, PACK], BF16, name="w_grouped_1", tag="reused_late", align_bytes=64),
-        ]
+        w_grouped = [held.tile([P, P, PACK], BF16, name=f"w_grouped_{h}", align_bytes=64) for h in range(2)]
 
         def listed(lo, hi):
             return offsets[:, CHUNK * lo // 16 : CHUNK * hi // 16]
@@ -75,21 +72,20 @@ def tile_attend_edge_uniq_bias_kernel(tc, xT, w, bias, offs, out):
 
         def place(u):
             nc.scalar.copy(
-                x_upper[:, CHUNK:, 2 * u : 2 * u + 2],
+                x_all[:, 3 * CHUNK :, 2 * u : 2 * u + 2],
                 flat[:, 2 * u : 2 * u + 2, :].rearrange("p e c -> p c e"),
             )
 
-        def w_views(h):
-            dst = w_grouped[h][:].rearrange("p (c i) t -> p c t i", i=4)
-            src = raw_w[h][:].rearrange("p t (c i) -> p c t i", i=4)
-            return dst, src
-
-        def quantize(name, values, tag=None):
-            width = values.shape[1]
+        def planes(name, width, tag=None):
             codes = held.tile([P, width], U32, name=f"{name}_codes", tag=tag or f"{name}_codes", align_bytes=64)
             scales = held.tile([P, width], U8, name=f"{name}_scales", align_bytes=64)
-            nc.vector.quantize_mx(codes[:].bitcast(FP8X4), scales[:], values.rearrange("p c t -> p (c t)"))
-            return codes[:], scales[:]
+            return [(codes[:, at : at + CHUNK], scales[:, at : at + CHUNK]) for at in range(0, width, CHUNK)]
+
+        def quantize(operand, values):
+            nc.vector.quantize_mx(operand[0].bitcast(FP8X4), operand[1], values.rearrange("p c t -> p (c t)"))
+
+        def quantize_x(c):
+            quantize(columns[c], x_all[:, CHUNK * c : CHUNK * c + CHUNK, :])
 
         for t in range(PACK - 1):
             gather_pairs(t, 0, 1)
@@ -103,14 +99,24 @@ def tile_attend_edge_uniq_bias_kernel(tc, xT, w, bias, offs, out):
         gather_flat(3)
         weave(0)
         place(1)
-        nc.vector.tensor_copy(*w_views(0))
-        nc.scalar.activation(*w_views(1), COPY)
+        nc.gpsimd.tensor_scalar(
+            w_grouped[0][:], raw_w[0][:].rearrange("p t c -> p c t"), 1.0, 0.0, op0=MULT, op1=ADD
+        )
+        nc.scalar.activation(
+            w_grouped[1][:].rearrange("p (c i) t -> p c t i", i=4),
+            raw_w[1][:].rearrange("p t (c i) -> p c t i", i=4),
+            COPY,
+        )
 
-        lower = quantize("lower", x_lower, tag="rows")
-        weights = [quantize("w_0", w_grouped[0][:])]
-        upper = quantize("upper", x_upper, tag="reused")
-        weights.append(quantize("w_1", w_grouped[1][:]))
-        third, last = [[plane[:, at : at + CHUNK] for plane in upper] for at in (0, CHUNK)]
+        weights = planes("w", M)
+        (first,) = planes("first", CHUNK)
+        later = planes("later", N - CHUNK, tag="reused")
+        columns = [later[0], first, later[1], later[2]]
+        quantize_x(1)
+        quantize(weights[0], w_grouped[0][:])
+        for c in (0, 2, 3):
+            quantize_x(c)
+        quantize(weights[1], w_grouped[1][:])
 
         def multiply(acc, h, operand):
             nc.tensor.matmul_mx(
@@ -129,13 +135,13 @@ def tile_attend_edge_uniq_bias_kernel(tc, xT, w, bias, offs, out):
             held.tile([P, G], F32, name="top_1", align_bytes=64),
         ]
 
-        def nodes(h, lo, operands):
-            widths = [operand[0].shape[1] for operand in operands]
-            acc = psum.tile([P, sum(widths)], F32, name=f"acc_{h}_{lo}")
-            for i, operand in enumerate(operands):
-                multiply(acc[:, sum(widths[:i]) : sum(widths[: i + 1])], h, operand)
-            hi = lo + sum(widths) // K
-            nc.vector.tensor_reduce(top[h][:, lo:hi], acc[:].rearrange("p (g j) -> p g j", j=K), AXIS_X, MAX)
+        def nodes(h, c):
+            acc = psum.tile([P, CHUNK], F32, name=f"acc_{h}_{c}")
+            multiply(acc[:], h, columns[c])
+            lo = CHUNK * c // K
+            nc.vector.tensor_reduce(
+                top[h][:, lo : lo + CHUNK // K], acc[:].rearrange("p (g j) -> p g j", j=K), AXIS_X, MAX
+            )
 
         def add_bias(h, lo, hi):
             nc.scalar.activation(res[:, h, lo:hi], top[h][:, lo:hi], IDENTITY, bias=bias_col[h][:])
@@ -144,11 +150,12 @@ def tile_attend_edge_uniq_bias_kernel(tc, xT, w, bias, offs, out):
             add_bias(h, lo, hi)
             nc.sync.dma_start(out_rows[:, h, lo:hi], res[:, h, lo:hi])
 
-        nodes(0, 0, [lower])
-        nodes(0, 64, [upper])
+        for c in (1, 0, 2, 3):
+            nodes(0, c)
         leave(0, 0, G)
-        nodes(1, 0, [lower])
+        nodes(1, 1)
+        nodes(1, 0)
         leave(1, 0, 64)
-        nodes(1, 64, [third])
-        nodes(1, 96, [last])
+        nodes(1, 2)
+        nodes(1, 3)
         leave(1, 64, G)

@@ -19,6 +19,7 @@ G, K, T, D, M = 128, 4, 1024, 512, 256
 N = G * K
 FLOPS = 2 * D * M * N
 CHUNK = 128
+VECTOR_SHARE = 32
 
 
 def tile_attend_edge_uniq_bias_kernel(tc, xT, w, bias, offs, out):
@@ -76,6 +77,11 @@ def tile_attend_edge_uniq_bias_kernel(tc, xT, w, bias, offs, out):
                 flat[:, 2 * u : 2 * u + 2, :].rearrange("p e c -> p c e"),
             )
 
+        def w_views(h, lo, hi):
+            dst = w_grouped[h][:, lo:hi, :].rearrange("p (c i) t -> p c t i", i=4)
+            src = raw_w[h][:, :, lo:hi].rearrange("p t (c i) -> p c t i", i=4)
+            return dst, src
+
         def planes(name, width, tag=None):
             codes = held.tile([P, width], U32, name=f"{name}_codes", tag=tag or f"{name}_codes", align_bytes=64)
             scales = held.tile([P, width], U8, name=f"{name}_scales", align_bytes=64)
@@ -102,11 +108,7 @@ def tile_attend_edge_uniq_bias_kernel(tc, xT, w, bias, offs, out):
         nc.gpsimd.tensor_scalar(
             w_grouped[0][:], raw_w[0][:].rearrange("p t c -> p c t"), 1.0, 0.0, op0=MULT, op1=ADD
         )
-        nc.scalar.activation(
-            w_grouped[1][:].rearrange("p (c i) t -> p c t i", i=4),
-            raw_w[1][:].rearrange("p t (c i) -> p c t i", i=4),
-            COPY,
-        )
+        nc.scalar.activation(*w_views(1, VECTOR_SHARE, P), COPY)
 
         weights = planes("w", M)
         (first,) = planes("first", CHUNK)
@@ -114,6 +116,7 @@ def tile_attend_edge_uniq_bias_kernel(tc, xT, w, bias, offs, out):
         columns = [later[0], first, later[1], later[2]]
         quantize_x(1)
         quantize(weights[0], w_grouped[0][:])
+        nc.vector.tensor_copy(*w_views(1, 0, VECTOR_SHARE))
         for c in (0, 2, 3):
             quantize_x(c)
         quantize(weights[1], w_grouped[1][:])

@@ -19,7 +19,9 @@ G, K, T, D, M = 128, 4, 1024, 512, 256
 N = G * K
 FLOPS = 2 * D * M * N
 CHUNK = 128
-VECTOR_SHARE = 32
+NODES = CHUNK // K
+GPSIMD_COLUMNS = 96
+VECTOR_COLUMNS = 32
 
 
 def tile_attend_edge_uniq_bias_kernel(tc, xT, w, bias, offs, out):
@@ -35,8 +37,8 @@ def tile_attend_edge_uniq_bias_kernel(tc, xT, w, bias, offs, out):
         offsets = held.tile([P, N // 16], U16, name="offsets")
         raw = [held.tile([P, T], F32, name=f"raw_{t}", align_bytes=64) for t in range(PACK)]
         raw_w = [
-            held.tile([P, PACK, P], F32, name="raw_w_0", tag="reused", align_bytes=64),
-            held.tile([P, PACK, P], F32, name="raw_w_1", tag="reused_late", align_bytes=64),
+            held.tile([P, PACK, P], F32, name="raw_w_0", tag="first_half", align_bytes=64),
+            held.tile([P, PACK, P], F32, name="raw_w_1", tag="second_half", align_bytes=64),
         ]
         bias_col = [held.tile([P, 1], F32, name=f"bias_col_{h}") for h in range(2)]
 
@@ -46,24 +48,17 @@ def tile_attend_edge_uniq_bias_kernel(tc, xT, w, bias, offs, out):
             nc.sync.dma_start(raw[t][:], x_rows[:, t, :])
         for h in range(2):
             nc.sync.dma_start(raw_w[h][:], w_rows[:, :, P * h : P * h + P])
-        for h in range(2):
-            nc.sync.dma_start(bias_col[h][:], bias[P * h : P * h + P, :])
+        for h, step in ((0, 32), (1, 64)):
+            for lo in range(0, P, step):
+                nc.sync.dma_start(bias_col[h][lo : lo + step, :], bias[P * h + lo : P * h + lo + step, :])
 
         flat = held.tile([P, PACK, CHUNK], BF16, name="flat", align_bytes=64)
-        pairs = held.tile([P, 1, 2, CHUNK, 2], BF16, name="pairs", align_bytes=64)
+        pairs = held.tile([P, CHUNK, 2], BF16, name="pairs", align_bytes=64)
         x_all = held.tile([P, N, PACK], BF16, name="x_all", align_bytes=64)
         w_grouped = [held.tile([P, P, PACK], BF16, name=f"w_grouped_{h}", align_bytes=64) for h in range(2)]
 
         def listed(lo, hi):
             return offsets[:, CHUNK * lo // 16 : CHUNK * hi // 16]
-
-        def gather_pairs(t, lo, hi):
-            nc.vector.tensor_copy(pairs[:, lo:hi, t // 2, :, t % 2], raw[t][:].indirect(listed(lo, hi)))
-
-        def weave(c):
-            dst = x_all[:, CHUNK * c : CHUNK * c + CHUNK, :].rearrange("p c t -> p (c t)").bitcast(U32)
-            src = pairs[:, c].rearrange("p u c e -> p (u c e)").bitcast(U32)
-            nc.scalar.copy(dst.rearrange("p (c u) -> p c u", u=2), src.rearrange("p (u c) -> p c u", u=2))
 
         def gather_direct(t, lo, hi):
             nc.vector.tensor_copy(x_all[:, CHUNK * lo : CHUNK * hi, t], raw[t][:].indirect(listed(lo, hi)))
@@ -71,11 +66,8 @@ def tile_attend_edge_uniq_bias_kernel(tc, xT, w, bias, offs, out):
         def gather_flat(t):
             nc.scalar.activation(flat[:, t, :], raw[t][:].indirect(listed(3, 4)), COPY)
 
-        def place(u):
-            nc.scalar.copy(
-                x_all[:, 3 * CHUNK :, 2 * u : 2 * u + 2],
-                flat[:, 2 * u : 2 * u + 2, :].rearrange("p e c -> p c e"),
-            )
+        def place_views(u):
+            return x_all[:, 3 * CHUNK :, 2 * u : 2 * u + 2], flat[:, 2 * u : 2 * u + 2, :].rearrange("p e c -> p c e")
 
         def w_views(h, lo, hi):
             dst = w_grouped[h][:, lo:hi, :].rearrange("p (c i) t -> p c t i", i=4)
@@ -93,71 +85,72 @@ def tile_attend_edge_uniq_bias_kernel(tc, xT, w, bias, offs, out):
         def quantize_x(c):
             quantize(columns[c], x_all[:, CHUNK * c : CHUNK * c + CHUNK, :])
 
-        for t in range(PACK - 1):
-            gather_pairs(t, 0, 1)
+        for t in range(2):
+            nc.vector.tensor_copy(pairs[:, :, t], raw[t][:].indirect(listed(0, 1)))
             gather_direct(t, 1, 3)
             gather_flat(t)
-            if t == 1:
-                place(0)
-        gather_pairs(3, 0, 1)
-        gather_direct(3, 1, 2)
-        gather_direct(3, 2, 3)
+        first_words = x_all[:, 0:CHUNK, :].rearrange("p c t -> p (c t)").bitcast(U32).rearrange("p (c u) -> p c u", u=2)
+        nc.scalar.copy(first_words[:, :, 0], pairs[:].rearrange("p c e -> p (c e)").bitcast(U32))
+        nc.gpsimd.tensor_scalar(*place_views(0), 1.0, 0.0, op0=MULT, op1=ADD)
+        gather_direct(2, 0, 3)
+        gather_flat(2)
+        for c in (1, 2, 0):
+            gather_direct(3, c, c + 1)
         gather_flat(3)
-        weave(0)
-        place(1)
+        nc.scalar.copy(*place_views(1))
         nc.gpsimd.tensor_scalar(
-            w_grouped[0][:], raw_w[0][:].rearrange("p t c -> p c t"), 1.0, 0.0, op0=MULT, op1=ADD
+            w_grouped[0][:, 0:GPSIMD_COLUMNS, :],
+            raw_w[0][:, :, 0:GPSIMD_COLUMNS].rearrange("p t c -> p c t"),
+            1.0,
+            0.0,
+            op0=MULT,
+            op1=ADD,
         )
-        nc.scalar.activation(*w_views(1, VECTOR_SHARE, P), COPY)
+        nc.scalar.activation(*w_views(0, GPSIMD_COLUMNS, P), COPY)
+        nc.scalar.activation(*w_views(1, VECTOR_COLUMNS, P), COPY)
 
         weights = planes("w", M)
-        (first,) = planes("first", CHUNK)
-        later = planes("later", N - CHUNK, tag="reused")
-        columns = [later[0], first, later[1], later[2]]
+        early = planes("early", 2 * CHUNK)
+        later = planes("later", 2 * CHUNK, tag="first_half")
+        columns = [later[0], early[0], early[1], later[1]]
         quantize_x(1)
+        quantize_x(2)
         quantize(weights[0], w_grouped[0][:])
-        nc.vector.tensor_copy(*w_views(1, 0, VECTOR_SHARE))
-        for c in (0, 2, 3):
+        nc.vector.tensor_copy(*w_views(1, 0, VECTOR_COLUMNS))
+        for c in (0, 3):
             quantize_x(c)
         quantize(weights[1], w_grouped[1][:])
 
-        def multiply(acc, h, operand):
-            nc.tensor.matmul_mx(
-                out=acc,
-                lhsT=weights[h][0].bitcast(FP8X4),
-                lhsT_scale=weights[h][1],
-                rhs=operand[0].bitcast(FP8X4),
-                rhs_scale=operand[1],
-                start=True,
-                stop=True,
-            )
-
         res = held.tile([P, 2, G], F32, name="res")
         top = [
-            held.tile([P, G], F32, name="top_0", tag="reused_late", align_bytes=64),
+            held.tile([P, G], F32, name="top_0", tag="second_half", align_bytes=64),
             held.tile([P, G], F32, name="top_1", align_bytes=64),
         ]
 
         def nodes(h, c):
             acc = psum.tile([P, CHUNK], F32, name=f"acc_{h}_{c}")
-            multiply(acc[:], h, columns[c])
-            lo = CHUNK * c // K
+            nc.tensor.matmul_mx(
+                out=acc[:],
+                lhsT=weights[h][0].bitcast(FP8X4),
+                lhsT_scale=weights[h][1],
+                rhs=columns[c][0].bitcast(FP8X4),
+                rhs_scale=columns[c][1],
+                start=True,
+                stop=True,
+            )
             nc.vector.tensor_reduce(
-                top[h][:, lo : lo + CHUNK // K], acc[:].rearrange("p (g j) -> p g j", j=K), AXIS_X, MAX
+                top[h][:, NODES * c : NODES * c + NODES], acc[:].rearrange("p (g j) -> p g j", j=K), AXIS_X, MAX
             )
 
-        def add_bias(h, lo, hi):
-            nc.scalar.activation(res[:, h, lo:hi], top[h][:, lo:hi], IDENTITY, bias=bias_col[h][:])
-
         def leave(h, lo, hi):
-            add_bias(h, lo, hi)
+            nc.scalar.activation(res[:, h, lo:hi], top[h][:, lo:hi], IDENTITY, bias=bias_col[h][:])
             nc.sync.dma_start(out_rows[:, h, lo:hi], res[:, h, lo:hi])
 
-        for c in (1, 0, 2, 3):
+        for c in (1, 2, 0, 3):
             nodes(0, c)
         leave(0, 0, G)
-        nodes(1, 1)
         nodes(1, 0)
+        nodes(1, 1)
         leave(1, 0, 64)
         nodes(1, 2)
         nodes(1, 3)

@@ -20,8 +20,10 @@ N = G * K
 FLOPS = 2 * D * M * N
 CHUNK = 128
 NODES = CHUNK // K
-GPSIMD_COLUMNS = 96
-VECTOR_COLUMNS = 32
+VECTOR_ENTRIES = 352
+SCALAR_CUT = 448
+GPSIMD_COLUMNS = 80
+VECTOR_COLUMNS = 48
 
 
 def tile_attend_edge_uniq_bias_kernel(tc, xT, w, bias, offs, out):
@@ -32,12 +34,13 @@ def tile_attend_edge_uniq_bias_kernel(tc, xT, w, bias, offs, out):
 
     with (
         tc.tile_pool(name="held", bufs=1) as held,
+        tc.tile_pool(name="shared", bufs=1) as shared,
         tc.psum_pool(name="psum", bufs=1) as psum,
     ):
         offsets = held.tile([P, N // 16], U16, name="offsets")
         raw = [held.tile([P, T], F32, name=f"raw_{t}", align_bytes=64) for t in range(PACK)]
         raw_w = [
-            held.tile([P, PACK, P], F32, name="raw_w_0", tag="first_half", align_bytes=64),
+            shared.tile([P, PACK, P], F32, name="raw_w_0", offset=0, align_bytes=64),
             held.tile([P, PACK, P], F32, name="raw_w_1", tag="second_half", align_bytes=64),
         ]
         bias_col = [held.tile([P, 1], F32, name=f"bias_col_{h}") for h in range(2)]
@@ -52,30 +55,33 @@ def tile_attend_edge_uniq_bias_kernel(tc, xT, w, bias, offs, out):
             for lo in range(0, P, step):
                 nc.sync.dma_start(bias_col[h][lo : lo + step, :], bias[P * h + lo : P * h + lo + step, :])
 
-        flat = held.tile([P, PACK, CHUNK], BF16, name="flat", align_bytes=64)
-        pairs = held.tile([P, CHUNK, 2], BF16, name="pairs", align_bytes=64)
+        flat = held.tile([P, PACK, N - VECTOR_ENTRIES], BF16, name="flat", align_bytes=64)
         x_all = held.tile([P, N, PACK], BF16, name="x_all", align_bytes=64)
-        w_grouped = [held.tile([P, P, PACK], BF16, name=f"w_grouped_{h}", align_bytes=64) for h in range(2)]
+        w_grouped = [
+            held.tile([P, P, PACK], BF16, name="w_grouped_0", align_bytes=64),
+            shared.tile([P, P, PACK], BF16, name="w_grouped_1", offset=1024, align_bytes=64),
+        ]
 
         def listed(lo, hi):
-            return offsets[:, CHUNK * lo // 16 : CHUNK * hi // 16]
+            return offsets[:, lo // 16 : hi // 16]
 
         def gather_direct(t, lo, hi):
-            nc.vector.tensor_copy(x_all[:, CHUNK * lo : CHUNK * hi, t], raw[t][:].indirect(listed(lo, hi)))
+            nc.vector.tensor_copy(x_all[:, lo:hi, t], raw[t][:].indirect(listed(lo, hi)))
 
-        def gather_flat(t):
-            nc.scalar.activation(flat[:, t, :], raw[t][:].indirect(listed(3, 4)), COPY)
+        def gather_flat(t, lo, hi):
+            rows = flat[:, t, lo - VECTOR_ENTRIES : hi - VECTOR_ENTRIES]
+            nc.scalar.activation(rows, raw[t][:].indirect(listed(lo, hi)), COPY)
 
-        def place_views(u):
-            return x_all[:, 3 * CHUNK :, 2 * u : 2 * u + 2], flat[:, 2 * u : 2 * u + 2, :].rearrange("p e c -> p c e")
+        def place_views(u, lo, hi):
+            rows = flat[:, 2 * u : 2 * u + 2, lo - VECTOR_ENTRIES : hi - VECTOR_ENTRIES]
+            return x_all[:, lo:hi, 2 * u : 2 * u + 2], rows.rearrange("p e c -> p c e")
 
         def w_views(h, lo, hi):
             dst = w_grouped[h][:, lo:hi, :].rearrange("p (c i) t -> p c t i", i=4)
             src = raw_w[h][:, :, lo:hi].rearrange("p t (c i) -> p c t i", i=4)
             return dst, src
 
-        def planes(name, width, tag=None):
-            codes = held.tile([P, width], U32, name=f"{name}_codes", tag=tag or f"{name}_codes", align_bytes=64)
+        def planes(name, width, codes):
             scales = held.tile([P, width], U8, name=f"{name}_scales", align_bytes=64)
             return [(codes[:, at : at + CHUNK], scales[:, at : at + CHUNK]) for at in range(0, width, CHUNK)]
 
@@ -85,19 +91,18 @@ def tile_attend_edge_uniq_bias_kernel(tc, xT, w, bias, offs, out):
         def quantize_x(c):
             quantize(columns[c], x_all[:, CHUNK * c : CHUNK * c + CHUNK, :])
 
-        for t in range(2):
-            nc.vector.tensor_copy(pairs[:, :, t], raw[t][:].indirect(listed(0, 1)))
-            gather_direct(t, 1, 3)
-            gather_flat(t)
-        first_words = x_all[:, 0:CHUNK, :].rearrange("p c t -> p (c t)").bitcast(U32).rearrange("p (c u) -> p c u", u=2)
-        nc.scalar.copy(first_words[:, :, 0], pairs[:].rearrange("p c e -> p (c e)").bitcast(U32))
-        nc.gpsimd.tensor_scalar(*place_views(0), 1.0, 0.0, op0=MULT, op1=ADD)
-        gather_direct(2, 0, 3)
-        gather_flat(2)
-        for c in (1, 2, 0):
-            gather_direct(3, c, c + 1)
-        gather_flat(3)
-        nc.scalar.copy(*place_views(1))
+        for t in range(PACK - 1):
+            gather_direct(t, 0, VECTOR_ENTRIES)
+            gather_flat(t, VECTOR_ENTRIES, N)
+            if t == 1:
+                nc.gpsimd.tensor_scalar(*place_views(0, VECTOR_ENTRIES, N), 1.0, 0.0, op0=MULT, op1=ADD)
+        gather_direct(3, CHUNK, VECTOR_ENTRIES)
+        gather_direct(3, 0, CHUNK)
+        pieces = ((VECTOR_ENTRIES, SCALAR_CUT), (SCALAR_CUT, N))
+        for lo, hi in pieces:
+            gather_flat(3, lo, hi)
+        for lo, hi in pieces:
+            nc.scalar.copy(*place_views(1, lo, hi))
         nc.gpsimd.tensor_scalar(
             w_grouped[0][:, 0:GPSIMD_COLUMNS, :],
             raw_w[0][:, :, 0:GPSIMD_COLUMNS].rearrange("p t c -> p c t"),
@@ -109,15 +114,15 @@ def tile_attend_edge_uniq_bias_kernel(tc, xT, w, bias, offs, out):
         nc.scalar.activation(*w_views(0, GPSIMD_COLUMNS, P), COPY)
         nc.scalar.activation(*w_views(1, VECTOR_COLUMNS, P), COPY)
 
-        weights = planes("w", M)
-        early = planes("early", 2 * CHUNK)
-        later = planes("later", 2 * CHUNK, tag="first_half")
-        columns = [later[0], early[0], early[1], later[1]]
+        weights = planes("w", M, held.tile([P, M], U32, name="w_codes", align_bytes=64))
+        early = planes("early", 2 * CHUNK, held.tile([P, 2 * CHUNK], U32, name="early_codes", align_bytes=64))
+        later = planes("later", 2 * CHUNK, shared.tile([P, 2 * CHUNK], U32, name="later_codes", offset=0, align_bytes=64))
+        columns = early + later
         quantize_x(1)
-        quantize_x(2)
+        quantize_x(0)
         quantize(weights[0], w_grouped[0][:])
         nc.vector.tensor_copy(*w_views(1, 0, VECTOR_COLUMNS))
-        for c in (0, 3):
+        for c in (2, 3):
             quantize_x(c)
         quantize(weights[1], w_grouped[1][:])
 
@@ -146,7 +151,7 @@ def tile_attend_edge_uniq_bias_kernel(tc, xT, w, bias, offs, out):
             nc.scalar.activation(res[:, h, lo:hi], top[h][:, lo:hi], IDENTITY, bias=bias_col[h][:])
             nc.sync.dma_start(out_rows[:, h, lo:hi], res[:, h, lo:hi])
 
-        for c in (1, 2, 0, 3):
+        for c in (1, 0, 2, 3):
             nodes(0, c)
         leave(0, 0, G)
         nodes(1, 0)

@@ -20,8 +20,6 @@ N = G * K
 FLOPS = 2 * D * M * N
 CHUNK = 128
 NODES = CHUNK // K
-VECTOR_ENTRIES = 352
-SCALAR_CUT = 448
 GPSIMD_COLUMNS = 80
 VECTOR_COLUMNS = 48
 
@@ -55,8 +53,9 @@ def tile_attend_edge_uniq_bias_kernel(tc, xT, w, bias, offs, out):
             for lo in range(0, P, step):
                 nc.sync.dma_start(bias_col[h][lo : lo + step, :], bias[P * h + lo : P * h + lo + step, :])
 
-        flat = held.tile([P, PACK, N - VECTOR_ENTRIES], BF16, name="flat", align_bytes=64)
-        x_all = held.tile([P, N, PACK], BF16, name="x_all", align_bytes=64)
+        flat = held.tile([P, PACK, CHUNK], BF16, name="flat", tag="rows", align_bytes=64)
+        pairs = held.tile([P, 2, CHUNK, 2], BF16, name="pairs", align_bytes=64)
+        x_rest = held.tile([P, N - CHUNK, PACK], BF16, name="x_rest", align_bytes=64)
         w_grouped = [
             held.tile([P, P, PACK], BF16, name="w_grouped_0", align_bytes=64),
             shared.tile([P, P, PACK], BF16, name="w_grouped_1", offset=1024, align_bytes=64),
@@ -65,16 +64,18 @@ def tile_attend_edge_uniq_bias_kernel(tc, xT, w, bias, offs, out):
         def listed(lo, hi):
             return offsets[:, lo // 16 : hi // 16]
 
+        def gather_pairs(t):
+            nc.vector.tensor_copy(pairs[:, t // 2, :, t % 2], raw[t][:].indirect(listed(0, CHUNK)))
+
         def gather_direct(t, lo, hi):
-            nc.vector.tensor_copy(x_all[:, lo:hi, t], raw[t][:].indirect(listed(lo, hi)))
+            nc.vector.tensor_copy(x_rest[:, lo - CHUNK : hi - CHUNK, t], raw[t][:].indirect(listed(lo, hi)))
 
         def gather_flat(t, lo, hi):
-            rows = flat[:, t, lo - VECTOR_ENTRIES : hi - VECTOR_ENTRIES]
-            nc.scalar.activation(rows, raw[t][:].indirect(listed(lo, hi)), COPY)
+            nc.scalar.activation(flat[:, t, lo:hi], raw[t][:].indirect(listed(3 * CHUNK + lo, 3 * CHUNK + hi)), COPY)
 
         def place_views(u, lo, hi):
-            rows = flat[:, 2 * u : 2 * u + 2, lo - VECTOR_ENTRIES : hi - VECTOR_ENTRIES]
-            return x_all[:, lo:hi, 2 * u : 2 * u + 2], rows.rearrange("p e c -> p c e")
+            rows = flat[:, 2 * u : 2 * u + 2, lo:hi]
+            return x_rest[:, 2 * CHUNK + lo : 2 * CHUNK + hi, 2 * u : 2 * u + 2], rows.rearrange("p e c -> p c e")
 
         def w_views(h, lo, hi):
             dst = w_grouped[h][:, lo:hi, :].rearrange("p (c i) t -> p c t i", i=4)
@@ -89,16 +90,18 @@ def tile_attend_edge_uniq_bias_kernel(tc, xT, w, bias, offs, out):
             nc.vector.quantize_mx(operand[0].bitcast(FP8X4), operand[1], values.rearrange("p c t -> p (c t)"))
 
         def quantize_x(c):
-            quantize(columns[c], x_all[:, CHUNK * c : CHUNK * c + CHUNK, :])
+            quantize(columns[c], x_rest[:, CHUNK * (c - 1) : CHUNK * c, :] if c else x_first[:])
 
         for t in range(PACK - 1):
-            gather_direct(t, 0, VECTOR_ENTRIES)
-            gather_flat(t, VECTOR_ENTRIES, N)
+            gather_pairs(t)
+            gather_direct(t, CHUNK, 3 * CHUNK)
+            gather_flat(t, 0, CHUNK)
             if t == 1:
-                nc.gpsimd.tensor_scalar(*place_views(0, VECTOR_ENTRIES, N), 1.0, 0.0, op0=MULT, op1=ADD)
-        gather_direct(3, CHUNK, VECTOR_ENTRIES)
-        gather_direct(3, 0, CHUNK)
-        pieces = ((VECTOR_ENTRIES, SCALAR_CUT), (SCALAR_CUT, N))
+                nc.gpsimd.tensor_scalar(*place_views(0, 0, CHUNK), 1.0, 0.0, op0=MULT, op1=ADD)
+        gather_direct(3, CHUNK, 2 * CHUNK)
+        gather_pairs(3)
+        gather_direct(3, 2 * CHUNK, 3 * CHUNK)
+        pieces = ((0, CHUNK // 2), (CHUNK // 2, CHUNK))
         for lo, hi in pieces:
             gather_flat(3, lo, hi)
         for lo, hi in pieces:
@@ -112,17 +115,22 @@ def tile_attend_edge_uniq_bias_kernel(tc, xT, w, bias, offs, out):
             op1=ADD,
         )
         nc.scalar.activation(*w_views(0, GPSIMD_COLUMNS, P), COPY)
+        x_first = held.tile([P, CHUNK, PACK], BF16, name="x_first", tag="rows", align_bytes=64)
+        nc.scalar.copy(
+            x_first[:].rearrange("p c t -> p (c t)").bitcast(U32).rearrange("p (c u) -> p c u", u=2),
+            pairs[:].rearrange("p u c e -> p (u c e)").bitcast(U32).rearrange("p (u c) -> p c u", u=2),
+        )
         nc.scalar.activation(*w_views(1, VECTOR_COLUMNS, P), COPY)
 
         weights = planes("w", M, held.tile([P, M], U32, name="w_codes", align_bytes=64))
         early = planes("early", 2 * CHUNK, held.tile([P, 2 * CHUNK], U32, name="early_codes", align_bytes=64))
         later = planes("later", 2 * CHUNK, shared.tile([P, 2 * CHUNK], U32, name="later_codes", offset=0, align_bytes=64))
-        columns = early + later
+        columns = [later[1], early[0], later[0], early[1]]
         quantize_x(1)
-        quantize_x(0)
+        quantize_x(3)
         quantize(weights[0], w_grouped[0][:])
         nc.vector.tensor_copy(*w_views(1, 0, VECTOR_COLUMNS))
-        for c in (2, 3):
+        for c in (2, 0):
             quantize_x(c)
         quantize(weights[1], w_grouped[1][:])
 
@@ -151,7 +159,7 @@ def tile_attend_edge_uniq_bias_kernel(tc, xT, w, bias, offs, out):
             nc.scalar.activation(res[:, h, lo:hi], top[h][:, lo:hi], IDENTITY, bias=bias_col[h][:])
             nc.sync.dma_start(out_rows[:, h, lo:hi], res[:, h, lo:hi])
 
-        for c in (1, 0, 2, 3):
+        for c in (1, 3, 2, 0):
             nodes(0, c)
         leave(0, 0, G)
         nodes(1, 0)

@@ -49,9 +49,9 @@ def tile_attend_edge_uniq_bias_kernel(tc, xT, w, bias, offs, out):
             nc.sync.dma_start(raw[t][:], x_rows[:, t, :])
         for h in range(2):
             nc.sync.dma_start(raw_w[h][:], w_rows[:, :, P * h : P * h + P])
-        for h, step in ((0, 32), (1, 64)):
-            for lo in range(0, P, step):
-                nc.sync.dma_start(bias_col[h][lo : lo + step, :], bias[P * h + lo : P * h + lo + step, :])
+        for h in range(2):
+            for lo in (0, P // 2):
+                nc.sync.dma_start(bias_col[h][lo : lo + P // 2, :], bias[P * h + lo : P * h + lo + P // 2, :])
 
         flat = held.tile([P, PACK, CHUNK], BF16, name="flat", tag="rows", align_bytes=64)
         pairs = held.tile([P, 2, CHUNK, 2], BF16, name="pairs", align_bytes=64)
@@ -155,16 +155,16 @@ def tile_attend_edge_uniq_bias_kernel(tc, xT, w, bias, offs, out):
                 top[h][:, NODES * c : NODES * c + NODES], acc[:].rearrange("p (g j) -> p g j", j=K), AXIS_X, MAX
             )
 
-        def leave(h, lo, hi):
+        def add_bias(h, lo, hi):
             nc.scalar.activation(res[:, h, lo:hi], top[h][:, lo:hi], IDENTITY, bias=bias_col[h][:])
-            nc.sync.dma_start(out_rows[:, h, lo:hi], res[:, h, lo:hi])
 
         for c in (1, 3, 2, 0):
             nodes(0, c)
-        leave(0, 0, G)
-        nodes(1, 0)
-        nodes(1, 1)
-        leave(1, 0, 64)
-        nodes(1, 2)
+            add_bias(0, NODES * c, NODES * c + NODES)
+            nc.sync.dma_start(out_rows[:, 0, NODES * c : NODES * c + NODES], res[:, 0, NODES * c : NODES * c + NODES])
+        for c in range(3):
+            nodes(1, c)
+        add_bias(1, 0, 3 * NODES)
         nodes(1, 3)
-        leave(1, 64, G)
+        add_bias(1, 3 * NODES, G)
+        nc.sync.dma_start(out_rows[:, 1, :], res[:, 1, :])

import concourse.mybir as mybir

F32 = mybir.dt.float32
BF16 = mybir.dt.bfloat16
U32 = mybir.dt.uint32
U16 = mybir.dt.uint16
U8 = mybir.dt.uint8
FP8X4 = mybir.dt.float8_e4m3fn_x4
COPY = mybir.ActivationFunctionType.Copy
IDENTITY = mybir.ActivationFunctionType.Identity
MULT = mybir.AluOpType.mult
ADD = mybir.AluOpType.add
MAX = mybir.AluOpType.max
AXIS_X = mybir.AxisListType.X

P = 128
PACK = 4
G, K, T, D, M = 128, 4, 1024, 512, 256
N = G * K
FLOPS = 2 * D * M * N
CHUNK = 128
NODES = CHUNK // K
GPSIMD_COLUMNS = 80
VECTOR_COLUMNS = 48


def tile_attend_edge_uniq_bias_kernel(tc, xT, w, bias, offs, out):
    nc = tc.nc
    x_rows = xT.rearrange("(p t) c -> p t c", t=PACK)
    w_rows = w.rearrange("(p t) m -> p t m", t=PACK)
    out_rows = out.rearrange("(h p) g -> p h g", h=2)

    with (
        tc.tile_pool(name="held", bufs=1) as held,
        tc.tile_pool(name="shared", bufs=1) as shared,
        tc.psum_pool(name="psum", bufs=1) as psum,
    ):
        offsets = held.tile([P, N // 16], U16, name="offsets")
        raw = [held.tile([P, T], F32, name=f"raw_{t}", align_bytes=64) for t in range(PACK)]
        raw_w = [
            shared.tile([P, PACK, P], F32, name="raw_w_0", offset=0, align_bytes=64),
            held.tile([P, PACK, P], F32, name="raw_w_1", tag="second_half", align_bytes=64),
        ]
        bias_col = [held.tile([P, 1], F32, name=f"bias_col_{h}") for h in range(2)]

        nc.sync.dma_start(raw[0][:], x_rows[:, 0, :])
        nc.sync.dma_start(offsets[:], offs)
        for t in range(1, PACK):
            nc.sync.dma_start(raw[t][:], x_rows[:, t, :])
        for h in range(2):
            nc.sync.dma_start(raw_w[h][:], w_rows[:, :, P * h : P * h + P])
        for h in range(2):
            for lo in (0, P // 2):
                nc.sync.dma_start(bias_col[h][lo : lo + P // 2, :], bias[P * h + lo : P * h + lo + P // 2, :])

        flat = held.tile([P, PACK, CHUNK], BF16, name="flat", tag="rows", align_bytes=64)
        pairs = held.tile([P, 2, CHUNK, 2], BF16, name="pairs", align_bytes=64)
        x_rest = held.tile([P, N - CHUNK, PACK], BF16, name="x_rest", align_bytes=64)
        w_grouped = [
            held.tile([P, P, PACK], BF16, name="w_grouped_0", align_bytes=64),
            shared.tile([P, P, PACK], BF16, name="w_grouped_1", offset=1024, align_bytes=64),
        ]

        def listed(lo, hi):
            return offsets[:, lo // 16 : hi // 16]

        def gather_pairs(t):
            nc.vector.tensor_copy(pairs[:, t // 2, :, t % 2], raw[t][:].indirect(listed(0, CHUNK)))

        def gather_direct(t, lo, hi):
            nc.vector.tensor_copy(x_rest[:, lo - CHUNK : hi - CHUNK, t], raw[t][:].indirect(listed(lo, hi)))

        def gather_flat(t, lo, hi):
            nc.scalar.activation(flat[:, t, lo:hi], raw[t][:].indirect(listed(3 * CHUNK + lo, 3 * CHUNK + hi)), COPY)

        def place_views(u, lo, hi):
            rows = flat[:, 2 * u : 2 * u + 2, lo:hi]
            return x_rest[:, 2 * CHUNK + lo : 2 * CHUNK + hi, 2 * u : 2 * u + 2], rows.rearrange("p e c -> p c e")

        def w_views(h, lo, hi):
            dst = w_grouped[h][:, lo:hi, :].rearrange("p (c i) t -> p c t i", i=4)
            src = raw_w[h][:, :, lo:hi].rearrange("p t (c i) -> p c t i", i=4)
            return dst, src

        def planes(name, width, codes):
            scales = held.tile([P, width], U8, name=f"{name}_scales", align_bytes=64)
            return [(codes[:, at : at + CHUNK], scales[:, at : at + CHUNK]) for at in range(0, width, CHUNK)]

        def quantize(operand, values):
            nc.vector.quantize_mx(operand[0].bitcast(FP8X4), operand[1], values.rearrange("p c t -> p (c t)"))

        def quantize_x(c):
            quantize(columns[c], x_rest[:, CHUNK * (c - 1) : CHUNK * c, :] if c else x_first[:])

        for t in range(PACK - 1):
            gather_pairs(t)
            gather_direct(t, CHUNK, 3 * CHUNK)
            gather_flat(t, 0, CHUNK)
            if t == 1:
                nc.gpsimd.tensor_scalar(*place_views(0, 0, CHUNK), 1.0, 0.0, op0=MULT, op1=ADD)
        gather_direct(3, CHUNK, 2 * CHUNK)
        gather_pairs(3)
        gather_direct(3, 2 * CHUNK, 3 * CHUNK)
        pieces = ((0, CHUNK // 2), (CHUNK // 2, CHUNK))
        for lo, hi in pieces:
            gather_flat(3, lo, hi)
        for lo, hi in pieces:
            nc.scalar.copy(*place_views(1, lo, hi))
        nc.gpsimd.tensor_scalar(
            w_grouped[0][:, 0:GPSIMD_COLUMNS, :],
            raw_w[0][:, :, 0:GPSIMD_COLUMNS].rearrange("p t c -> p c t"),
            1.0,
            0.0,
            op0=MULT,
            op1=ADD,
        )
        nc.scalar.activation(*w_views(0, GPSIMD_COLUMNS, P), COPY)
        x_first = held.tile([P, CHUNK, PACK], BF16, name="x_first", tag="rows", align_bytes=64)
        nc.scalar.copy(
            x_first[:].rearrange("p c t -> p (c t)").bitcast(U32).rearrange("p (c u) -> p c u", u=2),
            pairs[:].rearrange("p u c e -> p (u c e)").bitcast(U32).rearrange("p (u c) -> p c u", u=2),
        )
        nc.scalar.activation(*w_views(1, VECTOR_COLUMNS, P), COPY)

        weights = planes("w", M, held.tile([P, M], U32, name="w_codes", align_bytes=64))
        early = planes("early", 2 * CHUNK, held.tile([P, 2 * CHUNK], U32, name="early_codes", align_bytes=64))
        later = planes("later", 2 * CHUNK, shared.tile([P, 2 * CHUNK], U32, name="later_codes", offset=0, align_bytes=64))
        columns = [later[1], early[0], later[0], early[1]]
        quantize_x(1)
        quantize_x(3)
        quantize(weights[0], w_grouped[0][:])
        nc.vector.tensor_copy(*w_views(1, 0, VECTOR_COLUMNS))
        for c in (2, 0):
            quantize_x(c)
        quantize(weights[1], w_grouped[1][:])

        res = held.tile([P, 2, G], F32, name="res")
        top = [
            held.tile([P, G], F32, name="top_0", tag="second_half", align_bytes=64),
            held.tile([P, G], F32, name="top_1", align_bytes=64),
        ]

        def nodes(h, c):
            acc = psum.tile([P, CHUNK], F32, name=f"acc_{h}_{c}")
            nc.tensor.matmul_mx(
                out=acc[:],
                lhsT=weights[h][0].bitcast(FP8X4),
                lhsT_scale=weights[h][1],
                rhs=columns[c][0].bitcast(FP8X4),
                rhs_scale=columns[c][1],
                start=True,
                stop=True,
            )
            nc.vector.tensor_reduce(
                top[h][:, NODES * c : NODES * c + NODES], acc[:].rearrange("p (g j) -> p g j", j=K), AXIS_X, MAX
            )

        def add_bias(h, lo, hi):
            nc.scalar.activation(res[:, h, lo:hi], top[h][:, lo:hi], IDENTITY, bias=bias_col[h][:])

        for c in (1, 3, 2, 0):
            nodes(0, c)
            add_bias(0, NODES * c, NODES * c + NODES)
            nc.sync.dma_start(out_rows[:, 0, NODES * c : NODES * c + NODES], res[:, 0, NODES * c : NODES * c + NODES])
        for c in range(3):
            nodes(1, c)
        add_bias(1, 0, 3 * NODES)
        nodes(1, 3)
        add_bias(1, 3 * NODES, G)
        nc.sync.dma_start(out_rows[:, 1, :], res[:, 1, :])
